import numpy as np, ml_dtypes
CORES = [23,119,17,113]
N = 4
BF = ml_dtypes.bfloat16
V, P, L, RO, Q, CAP = 2688, 4096, 256, 3, 3, 64
H, ST = 2048, 10
MS, PO = (4, 4, 5, 5, 6, 6, 7, 8), 14
def rings(rng, hole):
    pool = 1 + np.argsort(rng.random((8, 16, 255)), axis=-1)[..., :PO]
    ms = np.stack([rng.permutation(np.array(MS)) for r in range(N)])
    pal = np.take_along_axis(np.broadcast_to(pool, (N, 8, 16, PO)), np.argsort(rng.random((N, 8, 16, PO)), axis=-1), 3)
    k = np.take_along_axis(pal, (rng.random((N, 8, 16, V)) * ms[:, :, None, None]).astype(np.int64), 3)
    u = rng.random((N, 8, 16, V))
    return np.where(u < hole, 0, np.where(u < hole + 0.05, rng.integers(1, 256, (N, 8, 16, V)), k))
def parts(rng, hole=0.12):
    t = rng.choice(np.array([0, 300, 500, 700, 850]), (N, 8, 16, 1)) + rng.integers(0, 100, (N, 8, 16, 1))
    return rings(rng, hole), rng.integers(0, V, (N, 8, 16, V)), rng.integers(0, 256, (N, 8, 16, P)), rng.integers(0, 256, (N, 8, 16, L)), t
def pack(k, b, x, z, t):
    def bf(a): return np.ascontiguousarray(a.reshape(N, 128, -1)).astype(np.float32).astype(BF)
    return {"ring": bf(k), "nbr": np.ascontiguousarray(b.reshape(N, 128, V)).astype(np.int32), "mat": bf(x), "z0": bf(z), "thr": np.ascontiguousarray(t.reshape(N, 128, 1)).astype(np.int32)}
def setup_inputs(rng):
    return pack(*parts(rng))
def setup_inputs_spread(rng):
    k, b, x, z, t = parts(rng)
    e = rng.integers(5, 13, (N, 8, 1, 1)); ix = np.minimum((255 * rng.random((N, 8, 16, V)) ** e).astype(np.int64), 254)
    keys = 1 + np.argsort(rng.random((8, 16, 255)), axis=-1)
    k = np.take_along_axis(np.broadcast_to(keys, (N, 8, 16, 255)), ix, 3)
    k = np.where(rng.random((N, 8, 16, V)) < rng.random((N, 8, 1, V)) ** 3, 0, k)
    b[:, ::2] = np.minimum((V * rng.random((N, 4, 16, V)) ** 2).astype(np.int64), V - 1)
    x = np.minimum((np.exp2(8 * rng.random((N, 8, 1, P))) * rng.random((N, 8, 16, P))).astype(np.int64), 255)
    z = np.minimum((np.exp2(8 * rng.random((N, 8, 1, L))) * rng.random((N, 8, 16, L))).astype(np.int64), 255)
    t = np.minimum(np.exp2(12 * rng.random((N, 8, 16, 1))).astype(np.int64), 4095)
    return pack(k, b, x, z, t)
def setup_inputs_ends(rng):
    k, b, x, z, t = parts(rng)
    c = rng.random((N, 8, 1, V)); dens = rng.choice(np.array([0.25, 0.25, 0.5]), (N, 8, 1, V))
    k = np.where(c < 0.25, 255, np.where(c < 0.4, 0, np.where(c < 0.85, 255 * (rng.random((N, 8, 16, V)) < dens), k)))
    k[:, 6, :, 2 * ST:ST * (L - 4):ST] = 255
    b = np.where(rng.random((N, 8, 16, V)) < 0.7, (V - 1) * rng.integers(0, 2, (N, 8, 16, V)), b)
    share = np.array([0.5, 0, 0.5, 0, 0, 0, 0, 0]).reshape(8, 1, 1)
    x = np.where(rng.random((N, 8, 1, P)) < share + 0.05, 255 * rng.integers(0, 2, (N, 8, 1, P)), 255 * rng.integers(0, 2, (N, 8, 16, P)))
    z = np.where(rng.random((N, 8, 1, L)) < share, 255 * rng.integers(0, 2, (N, 8, 1, L)), 255 * rng.integers(0, 2, (N, 8, 16, L)))
    t = np.broadcast_to(4095 * (rng.random((1, 8, 16, 1)) < 0.25), (N, 8, 16, 1)); t = np.where(rng.random((N, 8, 16, 1)) < 0.05, 4095 - t, t)
    t[:, 0, 0] = 4095; t[:, 7, 14] = 0; t[:, 7, 15] = 4095
    k[..., V - 1] = 255; k[..., 0] = 255 * (np.argsort(np.argsort(rng.random((N, 8, 16)), axis=-1), axis=-1) < 5)
    x[..., 0] = 0; x[..., P - 1] = 255
    p = np.arange(16)
    for lane in (1, L - 1):
        v = ST * lane; z[..., lane] = 255; k[..., v] = 0; b[:, :, 0, v] = V - 1
        x[..., ((255 * (2 * v + 1) >> 2) + 811 * p) & (P - 1)] = 0 if lane == 1 else 255 * ((p + 1) & 1)
    z[..., 0] = 0; z[..., L - 2] = 0; k[..., ST * (L - 2)] = 0
    a = (15 + Q) >> 1; v = ST * (L - 4); z[..., L - 4] = 0
    k[..., v] = 255 * (p < a); k[..., V - 2] = 255 * (p >= 16 - a); b[:, :, 0, v] = V - 2
    k[..., V - 3] = 255; k[..., V - 4] = 255; b[:, :, 0, V - 2] = V - 2
    for i, u in ((1, V - 1), (14, V - 3), (15, V - 4)): b[:, :, i, V - 2] = u
    return pack(k, b, x, z, t)
def setup_inputs_corners(rng):
    k, b, x, z, t = parts(rng)
    code = rng.integers(1, 256, (N, 8, 16, 1)); code[:, ::2] = code[:1, ::2]; row = np.arange(16)[:, None]
    u = rng.random((N, 8, 1, V))
    k = np.where((row < Q) | (u < 0.33), code, np.where(u < 0.66, rng.integers(1, 256, (N, 8, 16, V)), 0))
    own = np.broadcast_to(np.arange(V), (16, V)); many = (0, 1, CAP - 1, CAP, CAP + 1, L, CAP, L >> 1)
    for r in range(N):
        for g in range(8):
            n = many[(g + r) & 7]; lanes = rng.permutation(L)[:n]; vf = ST * lanes
            if g & 3 == 1: b[r, g] = np.where(rng.random((16, V)) < 0.5, own, b[r, g])
            if g & 3 == 2: b[r, g] = np.where(rng.random((16, V)) < 0.3, (V - 1) * rng.integers(0, 2, (16, V)), b[r, g])
            if g & 3 == 3: b[r, g] = np.where(rng.random((16, V)) < 0.5, rng.integers(0, V, (1, V)), b[r, g])
            gone = np.zeros(V, bool); gone[vf] = True
            b[r, g] = b[r, g] + gone[b[r, g]]
            if g & 3 == 1: b[r, g][:, vf[::2]] = vf[::2]
            k[r, g][:, vf] = np.where((row < Q - 1) & (rng.random(n) < 0.5), code[r, g], 0)
    t = np.where(rng.random((N, 8, 16, 1)) < 0.5, rng.choice(np.array([0, 1, 15, 600, 1000, 4095]), (N, 8, 16, 1)), t); t[:, ::2, :Q] = 0; t[:, 1, 15] = 4095
    x = np.where(rng.random((N, 8, 1, P)) < 0.2, rng.choice(np.array([0, 128, 255]), (N, 8, 1, P)), x)
    z = np.where(rng.random((N, 8, 1, L)) < 0.3, rng.choice(np.array([0, 1, 254, 255]), (N, 8, 1, L)), z)
    return pack(k, b, x, z, t)
def setup_inputs_crowd(rng):
    k, b, x, z, t = parts(rng, 0.22)
    k = np.where(rng.random((N, 8, 1, V)) < 0.03, 0, k)
    hubs = np.argsort(rng.random((N, 8, V)), axis=-1)[..., :12]
    h = np.take_along_axis(hubs, rng.integers(0, 12, (N, 8, 16 * V)), 2).reshape(N, 8, 16, V)
    b = np.where(rng.random((N, 8, 16, V)) < 0.6, h, b)
    x[:, 1::2] = np.take_along_axis(x[:, 1::2], np.broadcast_to(rng.integers(0, 8, (N, 4, 1, P)), (N, 4, 16, P)), 3)
    z[..., 1::2] = z[..., ::2]
    return pack(k, b, x, z, t)
def setup_inputs_far(rng):
    k, b, x, z, t = parts(rng); a = (15 + Q) >> 1; kk = np.arange(16)[:, None]
    up = rng.integers(0, 2, (N, 8, 1, 1)); up[0, 0] = 0; up[N - 1, 7] = 1
    x = rng.integers(0, 48, (N, 8, 16, P)) + 208 * up; z = rng.integers(0, 48, (N, 8, 16, L)) + 208 * (1 - up)
    t = np.where(rng.random((N, 8, 16, 1)) < 0.4, rng.integers(3000, 3500, (N, 8, 16, 1)), t)
    first = ST * np.arange(L); rest = np.setdiff1d(np.arange(V), first)
    for r in range(N):
        for g in range(8):
            if (g + r) & 1: continue
            code = rng.integers(1, 256, (16, 1)); o = rng.permutation(16)[:, None]
            rare = 1 + (code - 1 + rng.integers(1, 255, (16, V))) % 255
            other = np.where(rng.random((16, V)) < 0.7, 0, rare)
            u = rng.permutation(rest); q = len(u) >> 2; near = u[:q]; full = u[q:2 * q]; right = u[2 * q:3 * q]
            kr = k[r, g]; br = b[r, g]
            kr[:, first] = np.where(o < a, code, other[:, first])
            kr[:, right] = np.where(o >= 16 - a, code, other[:, right])
            kr[:, full] = code
            kr[:, near] = np.where(o == rng.integers(a, 16, q), rare[:, near], code)
            e = ST * rng.permutation(L)[:L >> 4]
            kr[:, e[::2]] = 0; kr[:, e[1::2]] = code
            br[:, first] = rng.choice(right, (16, L))
            i = rng.integers(0, 15, q); m = i + 1 + (rng.random(q) * (15 - i)).astype(np.int64)
            pick = rng.random((16, q)); low = rng.choice(near, (16, q)); top = rng.choice(full, (16, q)); poor = rng.choice(np.concatenate([first, u[2 * q:]]), (16, q))
            late = np.where((kk == m) | (pick < 0.4), top, np.where(pick < 0.7, low, poor))
            early = np.where((kk == i) | ((kk > i) & (pick < 0.5)), low, poor)
            br[:, right] = np.where(kk < m, early, late)
    return pack(k, b, x, z, t)
def check_inputs(d):
    bad = []
    for k, lo, hi in (("ring", 0, 255), ("nbr", 0, V - 1), ("mat", 0, 255), ("z0", 0, 255), ("thr", 0, 4095)):
        a = np.asarray(d[k]).astype(np.float64)
        if not (np.min(a) >= lo and np.max(a) <= hi): bad.append("range of " + k)
        elif np.any(a != np.floor(a)): bad.append("whole numbers in " + k)
    return bad
def columns(a, ix):
    return np.take_along_axis(a, ix[:, :, None, :], 3)
def by_lane(a):
    return np.ascontiguousarray(a.transpose(0, 1, 3, 2)).reshape(N, 8, L * 16)
def reference(ring, nbr, mat, z0, thr):
    K = ring.astype(np.float32).astype(np.int64).reshape(N, 8, 16, V); B = nbr.astype(np.int64).reshape(N, 8, 16, V)
    X = mat.astype(np.float32).astype(np.int64).reshape(N, 8, 16, P); z = z0.astype(np.float32).astype(np.int64).reshape(N, 8, 16, L)
    th = thr.astype(np.int64).reshape(N, 8, 16, 1); v = np.array(np.broadcast_to(ST * np.arange(L), (N, 8, L)))
    failures = np.zeros(N, np.int64); rv_old = np.zeros((N, 8, 16), np.int64); row = np.arange(16)[:, None]
    for t in range(RO):
        j = (np.sum(z, axis=2) + t) & 15
        n = np.take_along_axis(columns(B, v), j[:, :, None, :], 2)[:, :, 0]
        Kv = columns(K, v); Kn = columns(K, n)
        direct = np.sum((Kv == Kn) & (Kv > 0), axis=2) >= Q
        cand = by_lane(columns(B, n)); Kc = columns(K, cand).reshape(N, 8, 16, L, 16)
        score = np.minimum(np.sum((Kc == Kv[..., None]) & (Kc > 0), axis=2), np.sum((Kc == Kn[..., None]) & (Kc > 0), axis=2))
        k = np.argmax(score, axis=3)
        bridged = ~direct & (np.max(score, axis=3) >= Q); failed = ~direct & ~bridged
        w = np.where(bridged, np.take_along_axis(cand.reshape(N, 8, L, 16), k[..., None], 3)[..., 0], n)
        Kw = columns(K, w)
        place = (((Kw * (2 * v + 1)[:, :, None, :]) >> 2) + 811 * row + t) & (P - 1)
        Xc = columns(X, by_lane(place)).reshape(N, 8, 16, L, 16)
        d = np.sum(np.abs(Xc - z[..., None]), axis=2)
        p = np.argmin(d, axis=3)
        x = np.take_along_axis(Xc, p[:, :, None, :, None], 4)[..., 0]
        caught = (d.transpose(0, 1, 3, 2) < th + (failures & 15)[:, None, None, None]) & (Kw > 0)
        low = np.argmax(caught, axis=3)
        rv = np.where(np.any(caught, axis=3), np.take_along_axis(Kw, low[..., None], 3)[..., 0], 0)
        fi = failed.astype(np.int64); served = failed & (np.add.accumulate(fi, axis=2) - fi < CAP)
        h = np.sum(Kw * z, axis=2) & (H - 1)
        given = columns(np.roll(K, -1, axis=0), h)
        filled = np.where(Kv > 0, Kv, np.where(bridged[:, :, None, :], Kw, given))
        K2 = np.array(K); B2 = np.array(B); active = bridged | served
        for a in range(N):
            for g in range(8):
                i = np.nonzero(active[a, g])[0]
                u, first = np.unique(v[a, g, i], return_index=True); i = i[first]
                K2[a, g][:, u] = filled[a, g][:, i]
                i = i[bridged[a, g, i]]; B2[a, g, j[a, g, i], v[a, g, i]] = w[a, g, i]
        come = np.roll(rv_old, 1, axis=0)
        K = np.where((K2 == rv[..., None]) | (K2 == come[..., None]), 0, K2); B = B2
        z = (z + x) >> 1; v = w; rv_old = rv; failures = np.sum(fi, axis=(1, 2))
    return {"yk": K.reshape(N, 128, V).astype(np.float32).astype(BF), "yz": z.reshape(N, 128, L).astype(np.float32)}

@@ -1,0 +1,742 @@
+from concourse.mybir import AluOpType, AxisListType, ActivationFunctionType
+
+OP = AluOpType
+AF = ActivationFunctionType
+V, PL, L, NR, H = 2688, 4096, 256, 3, 2048
+REM = V + L
+NC, NL = 2, 128
+S17 = float(2 ** 17)
+BIG = float(2 ** 20)
+CYC, PEC, VF, WK, GA, SCA = 0.83, 0.42, 10.0, 60.0, 1.5, 3.0
+BON, CLB = 2000.0, 15000.0
+NSV, NSN, SUBK, SUBX = 0, 0, 2, 2
+CBN = {}
+CHN = {}
+ALIAS = {}
+SCRATCH = {}
+
+
+def _lay(d, names):
+    o = 0
+    for nm, w in names:
+        d[nm] = (o, o + w)
+        o += w
+    return o
+
+
+def _small(big, dtype, names):
+    o = 0
+    for nm in names:
+        ALIAS[nm] = (big, o)
+        o += 32 if nm == "wfl" else 16
+    SCRATCH[big] = ("sbuf", [128, o], dtype)
+
+
+def _bufs(dtype, width, names):
+    for nm in names:
+        SCRATCH[nm] = ("sbuf", [128, width], dtype)
+
+
+CBW = _lay(CBN, [("u17", 144), ("u32", 144), ("u1", 144), ("bo1", 128), ("boh", 128), ("i1", 128), ("ih", 128),
+                 ("im", 128), ("imh", 128), ("i256", 128), ("kb", 128), ("pt", 128), ("io", 256), ("tri", 256)])
+CHW = _lay(CHN, [("u1", 144), ("bo1", 128), ("i1", 128), ("im", 128), ("on", 128), ("lt", 128), ("ones", 128),
+                 ("sl", 512), ("rq", 2048), ("pc", 8)])
+_bufs("bfloat16", REM, ("tab0", "tab1", "tab2", "tab3"))
+_bufs("bfloat16", H, ("rem0", "rem1", "rem2", "kc0", "kc1", "e10", "e11", "e20", "e21", "xc0", "xc1", "mx0", "mx1", "da0",
+                      "da1", "db0", "db1"))
+_bufs("bfloat16", V, ("cln", "clb", "fin"))
+_bufs("bfloat16", L, ("zi", "zb", "kv", "kn", "q0", "qa", "qb", "e0", "kw", "kwc", "src", "sa", "sb", "f1", "hb", "ug",
+                      "flr", "nfr", "kvr", "knp", "kvp", "fi", "ed", "cnb"))
+_bufs("float16", L, ("bv", "nm", "cdh", "wm", "vrh0", "vrh1"))
+_bufs("float32", L, ("row", "jr", "tmpc", "av", "val", "vt", "sc", "v2", "pz", "dt", "ds", "xm", "sz", "zs", "bn", "yzf"))
+_bufs("float32", 128, ("m32", "mxm", "mnm"))
+_bufs("int32", L, ("yi", "yj", "pi", "pj", "pk"))
+_bufs("uint16", L, ("cd", "pl"))
+_bufs("float32", 4, ("ra0", "ra1", "ra2", "rb0", "rb1", "rc0", "rc1"))
+_bufs("float32", 8, ("fs", "rr"))
+_bufs("int32", 8, ("ipc",))
+_small("smu", "uint16", ("nl", "pw", "sl2", "sl", "wl0", "wl1", "wl2"))
+_small("sm32", "float32", ("dk", "nk16", "tot", "th", "ns0", "dr", "ns", "iaw", "hH", "h2", "hx", "hy", "va", "vb", "nw",
+                            "wrt", "vmd", "sx", "sy", "pH", "wr0", "wr1", "wr2", "dum", "v0w"))
+_small("sm16", "float16", ("w16", "fl", "iah", "vah", "p16", "wfl"))
+SCRATCH["nb"] = ("sbuf", [128, REM], "int32")
+SCRATCH["X"] = ("sbuf", [128, PL], "bfloat16")
+SCRATCH["thi"] = ("sbuf", [128, 1], "int32")
+SCRATCH["cb"] = ("sbuf", [128, CBW], "bfloat16")
+SCRATCH["ch"] = ("sbuf", [128, CHW], "float16")
+SCRATCH["u1f"] = ("sbuf", [128, 144], "float32")
+SCRATCH["col"] = ("sbuf", [128, 64], "float32")
+SCRATCH["e3"] = ("sbuf", [128, 1920], "bfloat16")
+for _b in range(8):
+    SCRATCH["ps%d" % _b] = ("psum", [128, 512], "float32")
+SEMAPHORES = ["qv", "qs", "qp", "qg"] + ["d%d" % i for i in range(40)] \
+    + [a + str(i) for a in ("push", "pl", "rvs", "rvl", "rws", "rwl") for i in range(3)]
+
+
+def rank_program(g, core, T, topo):
+    rank = T.rank_of(core)
+    if rank is None:
+        return
+    nranks = len(T.cores)
+    nxt, prv = T.cores[(rank + 1) % nranks], T.cores[(rank - 1) % nranks]
+    ops, hist, ndma, bon, nb_ = [], {}, [0], [0.0], [0]
+
+    def A(name, lo, hi, st=1):
+        if name in ALIAS:
+            name, o = ALIAS[name]
+            lo, hi = lo + o, hi + o
+        ap = T[name][:, lo:hi] if st == 1 else T[name][:, lo:hi:st]
+        return ([(name, lo, hi)], ap, (hi - lo + st - 1) // st)
+
+    def cb(nm, lo=0, w=None):
+        o, e = CBN[nm]
+        return A("cb", o + lo, e if w is None else o + lo + w)
+
+    def ch(nm, lo=0, w=None):
+        o, e = CHN[nm]
+        return A("ch", o + lo, e if w is None else o + lo + w)
+
+    def U(nm, q, half=False):
+        return (ch if half else cb)(nm, 15 - q, 128)
+
+    def ind(win, lst):
+        return (win[0] + lst[0], win[1].indirect(lst[1]), 16 * lst[2], 1)
+
+    def op(q, dur, rd, wr, call, sem=None, val=1, lat=0.0):
+        i = len(ops)
+        deps = {}
+        for regs, w in ((rd, 0), (wr, 1)):
+            for nm, lo, hi in regs:
+                if nm[:2] == "ps":
+                    for q2, j in hist.get(nm, {}).items():
+                        if j != i:
+                            deps[j] = deps.get(j, False) or q2 != q or q != "p"
+                else:
+                    for j, l2, h2, w2 in hist.get(nm, []):
+                        if j != i and l2 < hi and lo < h2 and (w or w2):
+                            deps[j] = True
+        for regs, w in ((rd, 0), (wr, 1)):
+            for nm, lo, hi in regs:
+                if nm[:2] == "ps":
+                    hist.setdefault(nm, {})[q] = i
+                else:
+                    a = hist.setdefault(nm, [])
+                    if w:
+                        a[:] = [e for e in a if e[0] == i or not (lo <= e[1] and e[2] <= hi)]
+                    a.append((i, lo, hi, w))
+        ops.append({"q": q, "dur": dur, "deps": deps, "call": call, "sem": sem, "val": val, "lat": lat, "bon": bon[0]})
+        return i
+
+    def vdur(n, f):
+        return max(64.0, n * f) * CYC + VF
+
+    def two(*xs):
+        return all(SCRATCH[x[0][0][0]][2] in ("bfloat16", "float16", "uint16") for x in xs)
+
+    def sc_(x):
+        return (x[1], x[0]) if isinstance(x, tuple) else (x, [])
+
+    def ts(out, a, s1, s2, o0, o1=None):
+        x1, r1 = sc_(s1)
+        x2, r2 = sc_(s2)
+        f = GA if len(a) > 3 else (0.5 if two(out, a) else 1.0)
+        if o1 is None:
+            def call():
+                return g.vector.tensor_scalar(out[1], a[1], x1, None, o0)
+        else:
+            def call():
+                return g.vector.tensor_scalar(out[1], a[1], x1, x2, o0, o1)
+        return op("v", vdur(a[2], f), a[0] + r1 + r2, out[0], call)
+
+    def tt(out, a, b, o):
+        ps = a[0][0][0][:2] == "ps" or b[0][0][0][:2] == "ps"
+        return op("v", vdur(b[2], GA if len(a) > 3 else 1.0 if ps else 2.0), a[0] + b[0], out[0],
+                  lambda: g.vector.tensor_tensor(out[1], a[1], b[1], o))
+
+    def cp(out, a):
+        f = SCA if len(out) > 3 else GA if len(a) > 3 else (0.5 if two(out, a) else 1.0)
+        wr = out[0][:1] if len(out) > 3 else out[0]
+        rd = a[0] + (out[0][1:] if len(out) > 3 else [])
+        return op("v", vdur(a[2], f), rd, wr, lambda: g.vector.tensor_copy(out[1], a[1]))
+
+    def red(out, a, o):
+        return op("v", vdur(a[2], 1.0), a[0], out[0], lambda: g.vector.tensor_reduce(out[1], a[1], AxisListType.X, o))
+
+    def scan(out, d0, d1, o0, o1):
+        return op("v", vdur(d1[2], 1.0), d0[0] + d1[0], out[0],
+                  lambda: g.vector.tensor_tensor_scan(out[1], d0[1], d1[1], 0.0, o0, o1))
+
+    def tr(out, a):
+        return op("v", vdur(a[2], 1.0), a[0], out[0], lambda: g.vector.transpose(out[1], a[1]))
+
+    def fill(out, c):
+        return op("v", vdur(out[2], 0.5), [], out[0], lambda: g.vector.memset(out[1], c))
+
+    def act(out, a, func=None, scale=1.0, bias=0.0):
+        x, r = sc_(bias)
+        fn = AF.Identity if func is None else func
+        return op("s", a[2] * (GA if len(a) > 3 else 1.0) * CYC + 60, a[0] + r, out[0],
+                  lambda: g.scalar.activation(out[1], a[1], fn, bias=x, scale=scale))
+
+    def mm(out, lhsT, rhs, start, stop):
+        f = 4 if SCRATCH[rhs[0][0][0]][2] == "float32" else 1
+        return op("p", max(min(64.0, lhsT[2]), rhs[2]) * f * PEC, lhsT[0] + rhs[0], out[0],
+                  lambda: g.tensor.matmul(out[1], lhsT[1], rhs[1], start, stop))
+
+    def group(out, pairs):
+        for i, pr in enumerate(pairs):
+            mm(pr[2] if len(pr) > 2 else out, pr[0], pr[1], i == 0, i == len(pairs) - 1)
+
+    def iota(out, pat, base, mul):
+        if SCRATCH[out[0][0][0]][2] != "int32":
+            def call():
+                return g.iota(out[1], pat, base, mul, allow_small_or_imprecise_dtypes=True)
+        else:
+            def call():
+                return g.iota(out[1], pat, base, mul)
+        return op("g", 130 + 2 * out[2] * CYC, [], out[0], call)
+
+    def dma(q, out, a, nbytes, add=False):
+        s = "d%d" % ndma[0]
+        ndma[0] += 1
+        eng = {"y": g.sync, "s": g.scalar, "g": g}[q]
+        if add:
+            def call():
+                return eng.dma_start(out[1], a[1], accum_op=OP.add)
+        else:
+            def call():
+                return eng.dma_start(out[1], a[1])
+        return op(q, 1000 if q == "g" else 60, a[0] + (out[0] if add else []), out[0], call, sem=s, val=16,
+                  lat=1900 + nbytes / 180.0)
+
+    def hbm(name, lo, hi):
+        return ([("hbm_" + name, lo, hi)], T[name][:, lo:hi], hi - lo)
+
+    def remote(dst, src, out, frm, rsem, lsem, nbytes):
+        rid, pid, _se = topo.addr(dst)
+        msk = topo.mask(core, dst)
+        ne = len(topo.engines(core, dst))
+        op("g", 1000, src[0], [], lambda: g.remote_dma(out[1], src[1], T.sem[rsem], T.sem[lsem], pid, rid, msk),
+           sem=lsem, val=ne, lat=2000 + nbytes / 60.0)
+        ops[-1]["remote"] = True
+        op("ext", 0, [], out[0], None, sem=rsem, val=len(topo.engines(frm, core)))
+        ops[-1]["after"] = len(ops) - 2
+
+    def KA(c, lo, hi, st=1): return A("ps%d" % c, lo, hi, st)
+    def AC(c, lo, hi): return A("ps%d" % (2 + c), lo, hi)
+    def SM(c, lo, hi, st=1): return A("ps%d" % (4 + c), lo, hi, st)
+    def DB(b, lo, hi): return A("ps%d" % (6 + b), lo, hi)
+    def F1(lo, hi): return A("ps1", 384 + lo, 384 + hi)
+    def col(i): return A("col", i, i + 1)
+    def ck(name, c): return A(name, NL * c, NL * c + NL)
+    def cw(name, c): return A(name, 8 * c, 8 * c + 8)
+    def fu(name): return A(name, 0, 16)
+    def tabw(t): return A("tab%d" % t, 0, V)
+    def zbuf(t): return "zi" if t == 0 else "zb"
+
+    dma("s", A("zi", 0, L), hbm("z0", 0, L), 2 * 128 * L)
+    dma("y", A("nb", 0, V), hbm("nbr", 0, V), 4 * 128 * V)
+    dma("s", A("tab0", 0, V), hbm("ring", 0, V), 2 * 128 * V)
+    dma("y", A("X", 0, PL), hbm("mat", 0, PL), 2 * 128 * PL)
+    dma("s", A("thi", 0, 1), hbm("thr", 0, 1), 512)
+    dma("y", A("tab1", 0, V), hbm("ring", 0, V), 2 * 128 * V)
+
+    iota(A("ipc", 0, 1), [[0, 1]], 0, 1)
+    iota(A("row", 0, 256), [[1, 256]], 0, 0)
+    iota(A("jr", 0, 256), [[0, 16], [1, 16]], 0, 0)
+    iota(A("m32", 0, 128), [[32, 4], [0, 32]], 0, 0)
+    iota(fu("dum"), [[16, 16]], V, 1)
+    iota(fu("v0w"), [[160, 16]], 0, 10)
+    iota(A("v2", 0, 256), [[20, 256]], 1, 0)
+    ip = A("ipc", 0, 1)
+    ts(A("ipc", 1, 2), ip, 15, None, OP.bitwise_and)
+    ts(A("ipc", 2, 3), ip, 96, None, OP.bitwise_and)
+    ts(A("ipc", 3, 4), ip, 4, 1, OP.logical_shift_right, OP.bitwise_and)
+    cp(A("col", 0, 2), A("ipc", 0, 2))
+    cp(A("col", 4, 6), A("ipc", 2, 4))
+    tt(col(2), col(0), col(1), OP.subtract)
+    ts(col(3), col(2), 15.0, None, OP.add)
+    for t in range(NR):
+        ts(col(36 + t), col(1), -1.0, float(16 + t), OP.mult, OP.add)
+        ts(col(8 + t), col(1), 3244.0, float(4 * t), OP.mult, OP.add)
+    row128 = A("row", 0, 128)
+    row144 = A("row", 0, 144)
+    j128 = A("jr", 0, 128)
+    tt(A("tmpc", 0, 256), A("row", 0, 256), A("jr", 0, 256), OP.subtract)
+    m16 = A("tmpc", 0, 128)
+    ts(cb("i1"), row128, col(0), None, OP.is_equal)
+    act(cb("im"), cb("i1"), AF.Copy, scale=-1.0)
+    ts(cb("bo1"), m16, col(2), None, OP.is_equal)
+    ts(ch("u1"), row144, col(3), None, OP.is_equal)
+    ts(ch("bo1"), m16, col(2), None, OP.is_equal)
+    ts(cb("u1"), row144, col(3), None, OP.is_equal)
+    act(cb("u17"), cb("u1"), AF.Copy, scale=S17)
+    ts(ch("i1"), row128, col(0), None, OP.is_equal)
+    ts(col(7), col(1), -4096.0, 61440.0 - 2.5 * S17, OP.mult, OP.add)
+    ts(cb("kb"), row128, 0.0, col(7), OP.mult, OP.add)
+    ts(A("mxm", 0, 128), j128, 0.5, 2e9, OP.is_ge, OP.mult)
+    ts(A("mxm", 0, 128), A("mxm", 0, 128), -1e9, None, OP.add)
+    for g2 in range(2):
+        for c2 in range(2):
+            k = 2 * g2 + c2
+            ts(col(24 + k), col(5), float(c2), 10000.0, OP.not_equal, OP.mult)
+            tt(col(28 + k), col(24 + k), col(0), OP.add)
+            ts(col(12 + k), col(28 + k), float(16 * (g2 - c2)), None, OP.add)
+            ts(ch("sl", 128 * k, 128), row128, col(12 + k), None, OP.is_equal)
+    act(cb("u32"), cb("u1"), AF.Copy, scale=32.0)
+    ts(col(6), col(1), -8.0, None, OP.add)
+    ts(cb("pt"), row128, 0.0, col(6), OP.mult, OP.add)
+    ts(A("mnm", 0, 128), A("mxm", 0, 128), -1.0, None, OP.mult)
+    ts(cb("io"), A("row", 0, 256), 512.0, None, OP.mult)
+    fill(col(16), BIG)
+    ts(fu("dum"), fu("dum"), col(2), None, OP.subtract)
+    ts(col(17), col(2), -10.0, None, OP.mult)
+    ts(fu("v0w"), fu("v0w"), col(17), None, OP.add)
+    ts(ch("pc"), A("dum", 0, 8), 16.0, float(8 - 16 * V), OP.mult, OP.add)
+    ts(A("u1f", 0, 144), row144, col(3), None, OP.is_equal)
+    ts(ch("on"), A("m32", 0, 128), col(4), None, OP.is_equal)
+    ts(ch("lt"), row128, col(0), None, OP.is_ge)
+    tt(ch("lt"), ch("lt"), ch("on"), OP.mult)
+    ts(ch("ones"), row128, 0.0, 1.0, OP.mult, OP.add)
+    for q in range(16):
+        ts(col(40 + q), col(1), float(q), None, OP.is_equal)
+    for q in range(16):
+        ts(ch("rq", 128 * q, 128), ch("bo1"), col(40 + q), None, OP.mult)
+    for nm in ("tab1", "tab2", "tab3"):
+        fill(A(nm, V, REM), 0.0)
+    fill(A("nb", V, REM), 0)
+    cp(col(18), A("thi", 0, 1))
+    ts(col(19), col(18), 32.0, None, OP.mult)
+    tt(col(22), col(19), col(6), OP.add)
+    ts(col(23), col(22), -BIG, BIG, OP.mult, OP.add)
+    ts(ch("im"), row128, col(0), -1.0, OP.is_equal, OP.mult)
+    act(cb("ih"), cb("i1"), AF.Copy, scale=0.5)
+    act(cb("imh"), cb("i1"), AF.Copy, scale=-0.5)
+    act(cb("i256"), cb("i1"), AF.Copy, scale=-256.0)
+    act(cb("boh"), cb("bo1"), AF.Copy, scale=0.5)
+    ts(cb("tri"), A("jr", 0, 256), col(1), 32768.0, OP.is_le, OP.mult)
+    remote(prv, A("tab0", 0, H), A("rem0", 0, H), nxt, "push0", "pl0", 2 * 128 * H)
+
+    def l2wrap(out, src, first=None):
+        (nm, lo, hi), (sn, slo, shi) = out, src
+        if first is not None:
+            mm(A(nm, lo, hi), first[0], first[1], True, False)
+        for c2 in range(2):
+            for g2 in range(2):
+                mm(A(nm, lo + c2, hi, 2), ch("sl", 128 * (2 * g2 + c2), 128), A(sn, slo + g2, shi, 2),
+                   first is None and g2 == 0, g2 == 1 and (first is None or c2 == 1))
+
+    def l2direct(c, o, nm, mats):
+        a = NL * c
+        big = "ch" if mats is ch else "cb"
+        lo = (CHN if mats is ch else CBN)["bo1"][0]
+        bank = "ps%d" % (4 + c)
+        for pa in range(4):
+            for ib in range(4):
+                out = ([(bank, 0, 1)], T[bank][32 * pa:32 * pa + 32, o + 2 * ib:o + 2 * ib + 2], 2)
+                mm(out, A(nm, a + 32 * ib, a + 32 * ib + 32), A(big, lo + 32 * pa, lo + 32 * pa + 32, 16), True, True)
+
+    def clean_q(t, c, nm):
+        x = ck(nm, c)
+        prs = [(cb("i1"), x)]
+        ts(ck("q0", c), x, 0.0, None, OP.is_equal)
+        prs.append((cb("im"), ck("q0", c)))
+        if t >= 2:
+            ts(ck("qb", c), x, A("rb0", 0, 1), A("rb0", 1, 2), OP.is_equal, OP.mult)
+            prs.append((cb("im"), ck("qb", c)))
+        if t >= 1:
+            ra = "ra%d" % (t - 1)
+            ts(ck("qa", c), x, A(ra, 0, 1), A(ra, 1, 2), OP.is_equal, OP.mult)
+            prs.append((cb("im"), ck("qa", c)))
+        return prs
+
+    def stage_v(t, c):
+        a = NL * c
+        if t == 0:
+            cp(ck("kv", c), A("tab0", 10 * a, 10 * (a + NL), 10))
+            ts(ck("bv", c), A("nb", 10 * a, 10 * (a + NL), 10), -1344.0, None, OP.add)
+        else:
+            vl = cw("wl%d" % (t - 1), c)
+            act(ck("kv", c), ind(tabw(t), vl))
+            ts(ck("bv", c), ind(A("nb", 0, V), vl), -1344.0, None, OP.add)
+        group(KA(c, 0, 128), clean_q(t, c, "kv"))
+
+    def stage_n(t, c):
+        a = NL * c
+        z = ck(zbuf(t), c)
+        m = AC(c, 128, 256)
+        mm(SM(c, 0, 128), cb("bo1" if t == 0 else "boh"), z, True, True)
+        mm(KA(c, 256, 384), cb("i1" if t == 0 else "ih"), z, True, True)
+        act(ck("zs", c), KA(c, 256, 384), bias=-0.5)
+        ts(ck("yi", c), SM(c, 0, 128), col(36 + t), None, OP.add)
+        ts(ck("yj", c), ck("yi", c), 15, None, OP.bitwise_and)
+        ts(m, ck("yj", c), 0.0, None, OP.is_equal)
+        tt(ck("nm", c), ck("bv", c), m, OP.mult)
+        group(SM(c, 128, 136), [(U("u1", q, True), A("nm", a + q, a + NL, 16)) for q in range(16)])
+        ts(cw("nl", c), SM(c, 128, 136), 1344.0, None, OP.add)
+        cp(ck("cd", c), ind(A("nb", 0, V), cw("nl", c)))
+        kc = "kc%d" % c
+        for s in range(SUBK):
+            act(A(kc, 2048 // SUBK * s, 2048 // SUBK * (s + 1)),
+                ind(tabw(t), A("cd", a + 128 // SUBK * s, a + 128 // SUBK * (s + 1))))
+        cp(ck("kn", c), ind(tabw(t), cw("nl", c)))
+        l2direct(c, 160, "nm", ch)
+        tt(ck("e0", c), ck("kn", c), KA(c, 0, 128), OP.is_equal)
+        l2direct(c, 168, "e0", cb)
+        ts(ck("cdh", c), ck("cd", c), -1344.0, None, OP.add)
+        group(KA(c, 128, 256), clean_q(t, c, "kn"))
+        if NSV:
+            act(ck("kvp", c), KA(c, 0, 128), AF.Copy)
+        if NSN:
+            act(ck("knp", c), KA(c, 128, 256), AF.Copy)
+        ts(cw("dk", c), SM(c, 168, 176), 2.5, 15 * S17, OP.is_ge, OP.mult)
+        tt(cw("nk16", c), cw("dk", c), SM(c, 160, 168), OP.add)
+
+    def stage_cmp(t, c):
+        kc = "kc%d" % c
+        a = NL * c
+        for e, db, ns, neg, lo in (("e1%d" % c, "da%d" % c, NSV, "kvp", 0), ("e2%d" % c, "db%d" % c, NSN, "knp", 128)):
+            out = SM(c, 384, 512) if lo == 0 else AC(c, 0, 128)
+            for b in range(ns // 4):
+                hi = 512 * (4 - b)
+                bk = nb_[0] % 2
+                nb_[0] += 1
+                for j in range(4):
+                    o = DB(bk, 128 * j, 128 * j + 128)
+                    mm(o, cb("i1"), A(kc, 12 - 4 * b + j, 2048, 16), True, False)
+                    mm(o, cb("im"), ck(neg, c), False, True)
+                act(A(db, hi - 512, hi), DB(bk, 0, 512), AF.Copy)
+                ts(A(e, hi - 512, hi), A(db, hi - 512, hi), 0.0, None, OP.is_equal)
+            mm(out, ch("i1"), ck("cdh", c), True, False)
+            mm(out, cb("i1"), cb("kb"), False, False)
+            for k in range(16):
+                ek = A(e, 128 * k, 128 * k + 128)
+                if k < 16 - ns:
+                    tt(ek, A(kc, k, 2048, 16), KA(c, lo, lo + 128), OP.is_equal)
+                mm(out, U("u17", k), ek, False, k == 15)
+            if lo == 0:
+                act(ck("av", c), out, AF.Copy)
+        act(ck("kvr", c), KA(c, 0, 128), AF.Relu)
+        tt(ck("val", c), ck("av", c), AC(c, 0, 128), OP.min)
+        tr(ck("vt", c), ck("val", c))
+        scan(ck("sc", c), A("mxm", 0, 128), ck("vt", c), OP.min, OP.max)
+        tt(cw("tot", c), A("sc", a + 15, a + NL, 16), cw("nk16", c), OP.max)
+        big = 1.5 * 2 ** 35
+        ts(cw("th", c), cw("tot", c), big, -big, OP.add, OP.add)
+        tt(cw("w16", c), cw("tot", c), cw("th", c), OP.subtract)
+        ts(cw("fl", c), cw("tot", c), 350000.0 - 2.5 * S17, None, OP.is_lt)
+        sm = "ps%d" % (4 + c)
+        l2wrap((sm, 136, 144), ("w16", 8 * c, 8 * c + 8))
+        l2wrap((sm, 144, 152), ("fl", 8 * c, 8 * c + 8))
+        ts(cw("wl%d" % t, c), SM(c, 136, 144), 1344.0, None, OP.add)
+        cp(A("wfl", 16 * c, 16 * c + 16), SM(c, 136, 152))
+        ts(cw("wr%d" % t, c), SM(c, 136, 144), 1344.0, None, OP.add)
+
+    def stage_w(t, c):
+        a = NL * c
+        cp(ck("kw", c), ind(tabw(t), cw("wl%d" % t, c)))
+        prs = [(cb("i1"), ck("kw", c))]
+        if t >= 1:
+            ra = A("ra%d" % (t - 1), 3, 4)
+            ts(ck("qa", c), ck("kw", c), ra, ra, OP.is_equal, OP.mult)
+            prs.append((cb("im"), ck("qa", c)))
+        if t >= 2:
+            rb = A("rb0", 0, 1)
+            ts(ck("qb", c), ck("kw", c), rb, rb, OP.is_equal, OP.mult)
+            prs.append((cb("im"), ck("qb", c)))
+        kw = SM(c, 0, 128)
+        group(kw, prs)
+        tt(ck("pi", c), ck("v2", c), kw, OP.mult)
+        ts(ck("pj", c), ck("pi", c), col(8 + t), None, OP.add)
+        ts(ck("pk", c), ck("pj", c), 2, PL - 1, OP.arith_shift_right, OP.bitwise_and)
+        cp(ck("pl", c), ck("pk", c))
+        for s in range(SUBX):
+            act(A("xc%d" % c, 2048 // SUBX * s, 2048 // SUBX * (s + 1)),
+                ind(A("X", 0, PL), A("pl", a + 128 // SUBX * s, a + 128 // SUBX * (s + 1))))
+        tt(ck("pz", c), ck(zbuf(t), c), kw, OP.mult)
+        act(ck("kwc", c), kw, AF.Copy)
+        act(ck("hb", c), ck("kwc", c), AF.Relu, scale=-BIG, bias=col(16))
+        for q in range(16):
+            mm(SM(c, 256 + q, 512, 16), ch("rq", 128 * q, 128), A("wfl", 16 * c, 16 * c + 16), True, True)
+        act(ck("flr", c), SM(c, 384, 512), scale=-512.0)
+        act(ck("nfr", c), SM(c, 384, 512), scale=512.0, bias=-512.0)
+        if t < NR - 1:
+            act(ck("v2", c), SM(c, 256, 384), scale=2.0, bias=2689.0)
+            vr = ck("vrh%d" % (t & 1), c)
+            cp(vr, SM(c, 256, 384))
+            tt(ck("wm", c), vr, AC(c, 128, 256), OP.mult)
+
+    def stage_full(t):
+        group(F1(0, 16), [(ch("lt"), fu("fl"))]
+              + [(ch("on"), A("fl", 0, 16 - 2 * d), F1(2 * d, 16)) for d in range(1, 8)])
+        mm(F1(16, 32), ch("ones"), fu("fl"), True, True)
+        ts(fu("ns0"), F1(0, 16), 64.5, None, OP.is_gt)
+        tt(fu("ns"), fu("ns0"), fu("fl"), OP.mult)
+        ts(fu("dr"), fu("tot"), 2.2e6 - 2.5 * S17, None, OP.is_gt)
+        tt(fu("iah"), fu("ns"), fu("dr"), OP.add)
+        l2wrap(("ps1", 432, 448), ("iah", 0, 16))
+        group(F1(64, 80), [(A("u1f", 15 - q, 143 - q), A("pz", q, L, 16)) for q in range(16)])
+        cp(fu("iaw"), F1(48, 64))
+        zs = 1.0 if t == 0 else 2.0
+        big = 1.5 * 2 ** 34 * zs
+        ts(fu("hH"), F1(64, 80), big, -big, OP.add, OP.add)
+        tt(fu("h2"), F1(64, 80), fu("hH"), OP.subtract)
+        ts(fu("hx"), fu("h2"), 0.0, H * zs, OP.is_lt, OP.mult)
+        tt(fu("hy"), fu("h2"), fu("hx"), OP.add)
+        ts(fu("sl2"), fu("hy"), 1.0 / zs, None, OP.mult)
+        tab = "tab%d" % (t + 1)
+        act(A("src", 0, L), ind(A("rem%d" % t, 0, H), fu("sl2")))
+        if t < NR - 1:
+            red(A("fs", 0, 1), F1(16, 32), OP.add)
+            ts(A("fs", 1, 2), A("fs", 0, 1), -7.5, None, OP.add)
+            b27 = 1.5 * 2 ** 27
+            ts(A("fs", 2, 3), A("fs", 1, 2), b27, -b27, OP.add, OP.add)
+            tt(A("fs", 3, 4), A("fs", 0, 1), A("fs", 2, 3), OP.subtract)
+        vw = fu("v0w") if t == 0 else fu("wr%d" % (t - 1))
+        tt(fu("vmd"), vw, fu("dum"), OP.subtract)
+        if t > 0:
+            ts(fu("va"), fu("iaw"), 16384.0, -1344.0, OP.mult, OP.add)
+            tt(fu("vb"), fu("va"), vw, OP.add)
+            cp(fu("vah"), fu("vb"))
+            vr = "vrh%d" % ((t - 1) & 1)
+            group(KA(0, 0, 256), [(cb("i1"), cb("tri"))]
+                  + [(ch("i1"), fu("vah"), KA(0, q, 256, 16)) for q in range(16)])
+            o = 0
+            prs = [(cb("bo1"), A("ed", 0, L))]
+            for c1 in range(15):
+                n = L - 16 * (c1 + 1)
+                ts(A("e3", o, o + n), A(vr, L - n, L), A("vb", c1, c1 + 1), None, OP.is_equal)
+                prs.append((cb("bo1"), A("e3", o, o + n), KA(1, 256 - n, 256)))
+                o += n
+            tt(A("ed", 0, L), A(vr, 0, L), KA(0, 0, 256), OP.is_equal)
+            group(KA(1, 0, 256), prs)
+            act(A("cnb", 0, L), KA(1, 0, 256), AF.Copy)
+            group(F1(80, 96), [(U("u1", q), A("cnb", q, L, 16)) for q in range(16)])
+            tt(fu("nw"), fu("iaw"), F1(80, 96), OP.add)
+            ts(fu("wrt"), fu("nw"), 0.5, None, OP.is_lt)
+        else:
+            ts(fu("wrt"), fu("iaw"), 0.5, None, OP.is_lt)
+        tt(fu("sx"), fu("wrt"), fu("vmd"), OP.mult)
+        tt(fu("sy"), fu("sx"), fu("dum"), OP.add)
+        cp(fu("sl"), fu("sy"))
+        for c in range(NC):
+            o = SM(c, 256, 384)
+            for x, fm in (("kwc", "flr"), ("src", "nfr")):
+                mm(o, cb("i1"), ck(x, c), True, False)
+                if x == "src" and t >= 1:
+                    ts(ck("sa", c), ck("src", c), A("rc%d" % (t - 1), 0, 1), A("rc%d" % (t - 1), 0, 1), OP.is_equal, OP.mult)
+                    mm(o, cb("im"), ck("sa", c), False, False)
+                if x == "src" and t >= 2:
+                    ts(ck("sb", c), ck("src", c), A("ra0", 0, 1), A("ra0", 0, 1), OP.is_equal, OP.mult)
+                    mm(o, cb("im"), ck("sb", c), False, False)
+                mm(o, cb("i1"), ck(fm, c), False, False)
+                mm(o, cb("i256"), ck("kvr", c), False, True)
+                tt(ck("f1" if x == "kwc" else "fi", c), ck("kvr" if x == "kwc" else "f1", c), o, OP.max)
+        cp(ind(A(tab, 0, REM), fu("sl")), A("fi", 0, L))
+        if t < NR - 1:
+            group(KA(0, 256, 512), [(ch("i1"), A("bv", 0, L)), (ch("im"), A("nm", 0, L)), (ch("i1"), A("wm", 0, L))])
+            act(A("bn", 0, L), KA(0, 256, 512), bias=1344.0)
+            cp(ind(A("nb", 0, REM), fu("sl")), A("bn", 0, L))
+            remote(prv, A(tab, 0, H), A("rem%d" % (t + 1), 0, H), nxt, "push%d" % (t + 1), "pl%d" % (t + 1), 2 * 128 * H)
+            dma("y", A("tab%d" % (t + 2), 0, V), A(tab, 0, V), 2 * 128 * V)
+
+    def stage_d(t, c):
+        a = NL * c
+        z = ck(zbuf(t), c)
+        out = AC(c, 256, 384)
+        xc = "xc%d" % c
+        mm(out, cb("i1"), cb("pt"), True, False)
+        for b in range(4):
+            bk = nb_[0] % 2
+            nb_[0] += 1
+            for j in range(4):
+                o = DB(bk, 128 * j, 128 * j + 128)
+                mm(o, cb("i1"), A(xc, 4 * b + j, 2048, 16), True, False)
+                mm(o, cb("im" if t == 0 else "imh"), z, False, True)
+            act(A("mx%d" % c, 512 * b, 512 * b + 512), DB(bk, 0, 512), AF.Abs)
+        for p in range(16):
+            mm(out, U("u32", p), A("mx%d" % c, 128 * p, 128 * p + 128), False, p == 15)
+        tr(ck("dt", c), out)
+        scan(ck("ds", c), A("mnm", 0, 128), ck("dt", c), OP.max, OP.min)
+        b28 = 1.5 * 2 ** 28
+        last = A("ds", a + 15, a + NL, 16)
+        ts(cw("pH", c), last, b28, -b28, OP.add, OP.add)
+        tt(cw("p16", c), last, cw("pH", c), OP.subtract)
+        l2wrap(("ps%d" % (4 + c), 152, 160), ("p16", 8 * c, 8 * c + 8), (ch("i1"), ch("pc")))
+        cp(cw("pw", c), SM(c, 152, 160))
+        tt(ck("sz", c), ind(A(xc, 0, 2048), cw("pw", c)), ck("zs", c), OP.add)
+        b24 = 1.5 * 2 ** 24
+        if t < NR - 1:
+            ts(ck("zb", c), ck("sz", c), b24, -b24, OP.add, OP.add)
+        else:
+            ts(ck("xm", c), ck("sz", c), b24, -b24, OP.add, OP.add)
+            act(ck("yzf", c), ck("xm", c), AF.Copy, scale=0.5)
+            dma("y", hbm("yz", a, a + NL), ck("yzf", c), 512 * NL)
+        tc = col(23) if t == 0 else A("fs", 4 + t, 5 + t)
+        act(ck("ug", c), out, AF.Relu, scale=BIG, bias=tc)
+        group(SM(c, 0, 128), [(cb("i1"), ck("kwc", c)), (cb("i1"), cb("io", a, NL)), (cb("i1"), ck("hb", c)),
+                              (cb("i1"), ck("ug", c))])
+        red(A("rr", c, c + 1), SM(c, 0, 128), OP.min)
+
+    BL = ((0, H), (H, V))
+
+    def clean(tab, frm, nm, acc):
+        bon[0] = -CLB
+        for lo, hi in BL:
+            ts(A(nm, lo, hi), A(frm, lo, hi), acc[0], acc[1], OP.is_equal, OP.mult)
+        for lo, hi in BL:
+            dma("g", A(tab, lo, hi), A(nm, lo, hi), 2 * 128 * (hi - lo) * 2, add=True)
+        bon[0] = 0.0
+
+    def stage_rv(t):
+        ra = "ra%d" % t
+        tt(A("rr", 2, 3), A("rr", 0, 1), A("rr", 1, 2), OP.min)
+        ts(A("rr", 2, 3), A("rr", 2, 3), BIG, None, OP.min)
+        b32 = 1.5 * 2 ** 32
+        ts(A("rr", 3, 4), A("rr", 2, 3), b32, -b32, OP.add, OP.add)
+        tt(A(ra, 0, 1), A("rr", 2, 3), A("rr", 3, 4), OP.subtract)
+        if t < NR - 1:
+            ts(A(ra, 1, 2), A(ra, 0, 1), 1.0, None, OP.add)
+            rb = "rb%d" % t
+            if t == 1:
+                tt(A("rr", 4, 5), A(ra, 0, 1), A("rb0", 0, 1), OP.not_equal)
+                tt(A(ra, 3, 4), A("rr", 4, 5), A(ra, 0, 1), OP.mult)
+            else:
+                cp(A(ra, 3, 4), A(ra, 0, 1))
+            ts(A(ra, 2, 3), A(ra, 3, 4), -1.0, None, OP.mult)
+            clean("tab%d" % (t + 2), "tab%d" % (t + 1), "cln", (A(ra, 3, 4), A(ra, 2, 3)))
+            remote(nxt, A(ra, 0, 2), A(rb, 0, 2), prv, "rvs%d" % t, "rvl%d" % t, 1024)
+            remote(prv, A(ra, 0, 2), A("rc%d" % t, 0, 2), nxt, "rws%d" % t, "rwl%d" % t, 1024)
+            ts(A(rb, 2, 3), A(rb, 0, 1), -1.0, None, OP.mult)
+        else:
+            tt(A("rr", 4, 5), A(ra, 0, 1), A("rb1", 0, 1), OP.not_equal)
+            tt(A("rr", 5, 6), A("rr", 4, 5), A(ra, 0, 1), OP.mult)
+            ts(A("rr", 6, 7), A("rr", 5, 6), -1.0, None, OP.mult)
+            for i in range(7):
+                lo, hi = 384 * i, 384 * i + 384
+                ts(A("cln", lo, hi), A("tab3", lo, hi), A("rr", 5, 6), A("rr", 6, 7), OP.is_equal, OP.mult)
+                o = A("ps%d" % (6, 7, 2, 3)[i % 4], 0, 384)
+                group(o, [(cb("i1"), A("tab3", lo, hi)), (cb("i1"), A("clb", lo, hi)), (cb("i1"), A("cln", lo, hi))])
+                if i % 2:
+                    cp(A("fin", lo, hi), o)
+                else:
+                    act(A("fin", lo, hi), o, AF.Copy)
+            for q, lo, hi in (("y", 0, 768), ("s", 768, 1536), ("y", 1536, 2304), ("s", 2304, V)):
+                dma(q, hbm("yk", lo, hi), A("fin", lo, hi), 256 * (hi - lo))
+
+    def st(f, t, c):
+        bon[0] = BON * (1 - c)
+        f(t, c)
+        bon[0] = 0.0
+
+    for t in range(NR):
+        for c in range(NC):
+            st(stage_v, t, c)
+            st(stage_n, t, c)
+        for c in range(NC):
+            st(stage_cmp, t, c)
+            st(stage_w, t, c)
+        stage_full(t)
+        if t == 1:
+            clean("tab3", "tab2", "clb", (A("rb0", 0, 1), A("rb0", 2, 3)))
+        if t == 2:
+            bon[0] = -CLB
+            for lo, hi in BL:
+                ts(A("clb", lo, hi), A("tab3", lo, hi), A("rb1", 0, 1), A("rb1", 2, 3), OP.is_equal, OP.mult)
+            bon[0] = 0.0
+        for c in range(NC):
+            st(stage_d, t, c)
+        if t < NR - 1:
+            ts(A("fs", 5 + t, 6 + t), A("fs", 3, 4), -32.0 * BIG, col(23), OP.mult, OP.add)
+        stage_rv(t)
+    _emit(g, T, ops)
+
+
+def _emit(g, T, ops):
+    n = len(ops)
+    succ = [[] for _ in range(n)]
+    for i, o in enumerate(ops):
+        if "after" in o:
+            o["deps"][o["after"]] = False
+        for j in o["deps"]:
+            succ[j].append(i)
+    prio = [0.0] * n
+    for i in range(n - 1, -1, -1):
+        o = ops[i]
+        prio[i] = o["dur"] + o["lat"] + max([prio[s] for s in succ[i]], default=0.0)
+    prio = [p + o["bon"] for p, o in zip(prio, ops)]
+    left = [len(o["deps"]) for o in ops]
+    fin = [0.0] * n
+    qfree, ready, order = {}, {}, []
+    est = [0.0] * n
+
+    def push(i):
+        o = ops[i]
+        e = 0.0
+        for j, hard in o["deps"].items():
+            if "after" in o and j == o["after"]:
+                e = max(e, fin[j])
+            elif hard:
+                e = max(e, fin[j] + WK)
+        est[i] = e
+        ready.setdefault(o["q"], []).append(i)
+    for i in range(n):
+        if left[i] == 0:
+            push(i)
+    while len(order) < n:
+        best = None
+        for q, rs in ready.items():
+            if not rs:
+                continue
+            f = 0.0 if q == "ext" else qfree.get(q, 0.0)
+            t0 = max(f, min(est[i] for i in rs))
+            if best is None or t0 < best[0]:
+                best = (t0, q)
+        t0, q = best
+        rs = ready[q]
+        i = max([i for i in rs if est[i] <= t0 + 30.0], key=lambda k: (prio[k], -k))
+        rs.remove(i)
+        o = ops[i]
+        st = max(t0, est[i])
+        qfree[q] = st + o["dur"]
+        fin[i] = st + o["dur"] + o["lat"]
+        order.append(i)
+        for s in succ[i]:
+            left[s] -= 1
+            if left[s] == 0:
+                push(s)
+    eng = {"v": g.vector, "s": g.scalar, "p": g.tensor, "g": g, "y": g.sync}
+    known = {q: {} for q in eng}
+    count, semof, clock = {}, {}, {}
+    pos = {i: k for k, i in enumerate(order)}
+    for i in order:
+        o = ops[i]
+        q = o["q"]
+        if q == "ext":
+            semof[i] = (o["sem"], o["val"])
+            count[o["sem"]] = o["val"]
+            clock[i] = {o["sem"]: o["val"]}
+            continue
+        kn = known[q]
+        need = {}
+        for j in sorted([j for j, hard in o["deps"].items() if hard], key=lambda j: -pos[j]):
+            s, v = semof[j]
+            if kn.get(s, 0) >= v:
+                continue
+            need[s] = max(need.get(s, 0), v)
+            for s2, v2 in clock[j].items():
+                if kn.get(s2, 0) < v2:
+                    kn[s2] = v2
+        for s, v in need.items():
+            eng[q].wait_ge(T.sem[s], v)
+        r = o["call"]()
+        s = "q" + q if o["sem"] is None else o["sem"]
+        count[s] = count.get(s, 0) + o["val"]
+        if "remote" not in o:
+            r.then_inc(T.sem[s], o["val"])
+        semof[i] = (s, count[s])
+        clock[i] = dict(kn)
+        clock[i][s] = count[s]
+    for s, v in count.items():
+        if known["g"].get(s, 0) < v:
+            g.wait_ge(T.sem[s], v)

@@ -7,11 +7,13 @@ REM = V + L
 NC, NL = 2, 128
 S17 = float(2 ** 17)
 BIG = float(2 ** 20)
-CYC, PEC, VF, WK, GA, SCA = 0.83, 0.42, 10.0, 60.0, 1.5, 3.0
-BON, CLB = 2000.0, 15000.0
-NSV, NSN, SUBK, SUBX = 0, 0, 2, 2
+CYC, PEC, VF, SF, WK, GA, SCA = 0.83, 0.42, 80.0, 100.0, 60.0, 1.5, 3.0
+CLB = 15000.0
+BT = {"v": (0.0, 0.0), "n": (1700.0, 0.0), "c": (2000.0, 0.0), "w": (8800.0, 600.0), "d": (3800.0, 700.0), "f": (0.0,)}
+CAP = 64
+NSB, E3S = 16, 0
+NSV, NSN, EQB, SUBK, SUBX = 0, 16, 1, 2, 2
 CBN = {}
-CHN = {}
 ALIAS = {}
 SCRATCH = {}
 
@@ -28,7 +30,7 @@ def _small(big, dtype, names):
     o = 0
     for nm in names:
         ALIAS[nm] = (big, o)
-        o += 32 if nm == "wfl" else 16
+        o += 32 if nm[:3] == "wfl" else 16
     SCRATCH[big] = ("sbuf", [128, o], dtype)
 
 
@@ -37,18 +39,20 @@ def _bufs(dtype, width, names):
         SCRATCH[nm] = ("sbuf", [128, width], dtype)
 
 
-CBW = _lay(CBN, [("u17", 144), ("u32", 144), ("u1", 144), ("bo1", 128), ("boh", 128), ("i1", 128), ("ih", 128),
-                 ("im", 128), ("imh", 128), ("i256", 128), ("kb", 128), ("pt", 128), ("io", 256), ("tri", 256)])
-CHW = _lay(CHN, [("u1", 144), ("bo1", 128), ("i1", 128), ("im", 128), ("on", 128), ("lt", 128), ("ones", 128),
-                 ("sl", 512), ("rq", 2048), ("pc", 8)])
+CBW = _lay(CBN, [("u17", 144), ("u32", 144), ("u1", 144), ("bo1", 128), ("boh", 128), ("i1", 128),
+                 ("im", 128), ("imh", 128), ("i256", 128), ("i1k", 128), ("kb", 128), ("pt", 128), ("io", 256), ("tri", 256),
+                 ("on", 128), ("lt", 128), ("ones", 128), ("sl", 512), ("rq", 2048), ("c13", 16), ("c75", 2),
+                 ("m512", 128), ("ih", 128), ("u64", 144), ("um32", 144), ("bv16", 128), ("bv32", 128)])
 _bufs("bfloat16", REM, ("tab0", "tab1", "tab2", "tab3"))
-_bufs("bfloat16", H, ("rem0", "rem1", "rem2", "kc0", "kc1", "e10", "e11", "e20", "e21", "xc0", "xc1", "mx0", "mx1", "da0",
+_bufs("bfloat16", H + 16, ("rem0", "rem1", "rem2"))
+_bufs("bfloat16", H, ("kc0", "kc1", "e10", "e11", "e20", "e21", "xc0", "xc1", "mx0", "mx1", "da0",
                       "da1", "db0", "db1"))
 _bufs("bfloat16", V, ("cln", "clb", "fin"))
 _bufs("bfloat16", L, ("zi", "zb", "kv", "kn", "q0", "qa", "qb", "e0", "kw", "kwc", "src", "sa", "sb", "f1", "hb", "ug",
                       "flr", "nfr", "kvr", "knp", "kvp", "fi", "ed", "cnb"))
-_bufs("float16", L, ("bv", "nm", "cdh", "wm", "vrh0", "vrh1"))
-_bufs("float32", L, ("row", "jr", "tmpc", "av", "val", "vt", "sc", "v2", "pz", "dt", "ds", "xm", "sz", "zs", "bn", "yzf"))
+_bufs("float16", L, ("bv", "nm", "cdh", "wm"))
+_bufs("float16", 8, ("pc",))
+_bufs("float32", L, ("wrp0", "wrp1", "row", "jr", "tmpc", "av", "val", "vt", "sc", "v2", "pz", "dt", "ds", "xm", "sz", "zs", "bn", "yzf"))
 _bufs("float32", 128, ("m32", "mxm", "mnm"))
 _bufs("int32", L, ("yi", "yj", "pi", "pj", "pk"))
 _bufs("uint16", L, ("cd", "pl"))
@@ -56,21 +60,19 @@ _bufs("float32", 4, ("ra0", "ra1", "ra2", "rb0", "rb1", "rc0", "rc1"))
 _bufs("float32", 8, ("fs", "rr"))
 _bufs("int32", 8, ("ipc",))
 _small("smu", "uint16", ("nl", "pw", "sl2", "sl", "wl0", "wl1", "wl2"))
-_small("sm32", "float32", ("dk", "nk16", "tot", "th", "ns0", "dr", "ns", "iaw", "hH", "h2", "hx", "hy", "va", "vb", "nw",
-                            "wrt", "vmd", "sx", "sy", "pH", "wr0", "wr1", "wr2", "dum", "v0w"))
-_small("sm16", "float16", ("w16", "fl", "iah", "vah", "p16", "wfl"))
+_small("sm32", "float32", ("dk", "nk16", "tot", "th", "hH", "h2", "vb", "sy", "pH", "dum", "v0w"))
+_small("sm16", "float16", ("w16", "fl", "dr", "iah", "vah", "p16", "wfl0", "wfl1"))
 SCRATCH["nb"] = ("sbuf", [128, REM], "int32")
 SCRATCH["X"] = ("sbuf", [128, PL], "bfloat16")
 SCRATCH["thi"] = ("sbuf", [128, 1], "int32")
 SCRATCH["cb"] = ("sbuf", [128, CBW], "bfloat16")
-SCRATCH["ch"] = ("sbuf", [128, CHW], "float16")
 SCRATCH["u1f"] = ("sbuf", [128, 144], "float32")
 SCRATCH["col"] = ("sbuf", [128, 64], "float32")
 SCRATCH["e3"] = ("sbuf", [128, 1920], "bfloat16")
 for _b in range(8):
     SCRATCH["ps%d" % _b] = ("psum", [128, 512], "float32")
 SEMAPHORES = ["qv", "qs", "qp", "qg"] + ["d%d" % i for i in range(40)] \
-    + [a + str(i) for a in ("push", "pl", "rvs", "rvl", "rws", "rwl") for i in range(3)]
+    + [a + str(i) for a in ("pusha", "pushb", "pla", "plb", "rvs", "rvl", "rws", "rwl") for i in range(3)]
 
 
 def rank_program(g, core, T, topo):
@@ -92,12 +94,8 @@ def rank_program(g, core, T, topo):
         o, e = CBN[nm]
         return A("cb", o + lo, e if w is None else o + lo + w)
 
-    def ch(nm, lo=0, w=None):
-        o, e = CHN[nm]
-        return A("ch", o + lo, e if w is None else o + lo + w)
-
-    def U(nm, q, half=False):
-        return (ch if half else cb)(nm, 15 - q, 128)
+    def U(nm, q):
+        return cb(nm, 15 - q, 128)
 
     def ind(win, lst):
         return (win[0] + lst[0], win[1].indirect(lst[1]), 16 * lst[2], 1)
@@ -174,9 +172,10 @@ def rank_program(g, core, T, topo):
 
     def act(out, a, func=None, scale=1.0, bias=0.0):
         x, r = sc_(bias)
+        y, r2 = sc_(scale)
         fn = AF.Identity if func is None else func
-        return op("s", a[2] * (GA if len(a) > 3 else 1.0) * CYC + 60, a[0] + r, out[0],
-                  lambda: g.scalar.activation(out[1], a[1], fn, bias=x, scale=scale))
+        return op("s", a[2] * (GA if len(a) > 3 else 1.0) * CYC + SF, a[0] + r + r2, out[0],
+                  lambda: g.scalar.activation(out[1], a[1], fn, bias=x, scale=y))
 
     def mm(out, lhsT, rhs, start, stop):
         f = 4 if SCRATCH[rhs[0][0][0]][2] == "float32" else 1
@@ -196,7 +195,7 @@ def rank_program(g, core, T, topo):
                 return g.iota(out[1], pat, base, mul)
         return op("g", 130 + 2 * out[2] * CYC, [], out[0], call)
 
-    def dma(q, out, a, nbytes, add=False):
+    def dma(q, out, a, nbytes, add=False, after=()):
         s = "d%d" % ndma[0]
         ndma[0] += 1
         eng = {"y": g.sync, "s": g.scalar, "g": g}[q]
@@ -206,7 +205,7 @@ def rank_program(g, core, T, topo):
         else:
             def call():
                 return eng.dma_start(out[1], a[1])
-        return op(q, 1000 if q == "g" else 60, a[0] + (out[0] if add else []), out[0], call, sem=s, val=16,
+        return op(q, 1000 if q == "g" else 60, a[0] + (out[0] if add else []) + [(x, 0, 1) for x in after], out[0], call, sem=s, val=16,
                   lat=1900 + nbytes / 180.0)
 
     def hbm(name, lo, hi):
@@ -237,9 +236,9 @@ def rank_program(g, core, T, topo):
     dma("s", A("zi", 0, L), hbm("z0", 0, L), 2 * 128 * L)
     dma("y", A("nb", 0, V), hbm("nbr", 0, V), 4 * 128 * V)
     dma("s", A("tab0", 0, V), hbm("ring", 0, V), 2 * 128 * V)
-    dma("y", A("X", 0, PL), hbm("mat", 0, PL), 2 * 128 * PL)
     dma("s", A("thi", 0, 1), hbm("thr", 0, 1), 512)
-    dma("y", A("tab1", 0, V), hbm("ring", 0, V), 2 * 128 * V)
+    dma("y", A("X", 0, PL), hbm("mat", 0, PL), 2 * 128 * PL, after=("nb", "tab0"))
+    dma("y", A("tab1", 0, V), hbm("ring", 0, V), 2 * 128 * V, after=("X",))
 
     iota(A("ipc", 0, 1), [[0, 1]], 0, 1)
     iota(A("row", 0, 256), [[1, 256]], 0, 0)
@@ -256,9 +255,8 @@ def rank_program(g, core, T, topo):
     cp(A("col", 4, 6), A("ipc", 2, 4))
     tt(col(2), col(0), col(1), OP.subtract)
     ts(col(3), col(2), 15.0, None, OP.add)
-    for t in range(NR):
-        ts(col(36 + t), col(1), -1.0, float(16 + t), OP.mult, OP.add)
-        ts(col(8 + t), col(1), 3244.0, float(4 * t), OP.mult, OP.add)
+    ts(col(36), col(1), -1.0, 16.0, OP.mult, OP.add)
+    ts(col(8), col(1), 3244.0, None, OP.mult)
     row128 = A("row", 0, 128)
     row144 = A("row", 0, 144)
     j128 = A("jr", 0, 128)
@@ -267,74 +265,82 @@ def rank_program(g, core, T, topo):
     ts(cb("i1"), row128, col(0), None, OP.is_equal)
     act(cb("im"), cb("i1"), AF.Copy, scale=-1.0)
     ts(cb("bo1"), m16, col(2), None, OP.is_equal)
-    ts(ch("u1"), row144, col(3), None, OP.is_equal)
-    ts(ch("bo1"), m16, col(2), None, OP.is_equal)
     ts(cb("u1"), row144, col(3), None, OP.is_equal)
     act(cb("u17"), cb("u1"), AF.Copy, scale=S17)
-    ts(ch("i1"), row128, col(0), None, OP.is_equal)
     ts(col(7), col(1), -4096.0, 61440.0 - 2.5 * S17, OP.mult, OP.add)
-    ts(cb("kb"), row128, 0.0, col(7), OP.mult, OP.add)
+    act(cb("kb"), row128, scale=0.0, bias=col(7))
     ts(A("mxm", 0, 128), j128, 0.5, 2e9, OP.is_ge, OP.mult)
     ts(A("mxm", 0, 128), A("mxm", 0, 128), -1e9, None, OP.add)
+    ts(col(12), col(5), 10000.0, col(0), OP.mult, OP.add)
+    ts(col(13), col(5), -10000.0, col(0), OP.mult, OP.add)
     for g2 in range(2):
         for c2 in range(2):
-            k = 2 * g2 + c2
-            ts(col(24 + k), col(5), float(c2), 10000.0, OP.not_equal, OP.mult)
-            tt(col(28 + k), col(24 + k), col(0), OP.add)
-            ts(col(12 + k), col(28 + k), float(16 * (g2 - c2)), None, OP.add)
-            ts(ch("sl", 128 * k, 128), row128, col(12 + k), None, OP.is_equal)
+            ts(cb("sl", 128 * (2 * g2 + c2), 128), row128, float(-16 * g2 if c2 == 0 else 16 * (1 - g2) - 10000), col(12 + c2),
+               OP.add, OP.is_equal)
     act(cb("u32"), cb("u1"), AF.Copy, scale=32.0)
     ts(col(6), col(1), -8.0, None, OP.add)
-    ts(cb("pt"), row128, 0.0, col(6), OP.mult, OP.add)
-    ts(A("mnm", 0, 128), A("mxm", 0, 128), -1.0, None, OP.mult)
-    ts(cb("io"), A("row", 0, 256), 512.0, None, OP.mult)
+    act(cb("pt"), row128, scale=0.0, bias=col(6))
+    act(A("mnm", 0, 128), A("mxm", 0, 128), AF.Copy, scale=-1.0)
+    iota(cb("io"), [[512, 256]], 0, 0)
     fill(col(16), BIG)
     ts(fu("dum"), fu("dum"), col(2), None, OP.subtract)
     ts(col(17), col(2), -10.0, None, OP.mult)
     ts(fu("v0w"), fu("v0w"), col(17), None, OP.add)
-    ts(ch("pc"), A("dum", 0, 8), 16.0, float(8 - 16 * V), OP.mult, OP.add)
-    ts(A("u1f", 0, 144), row144, col(3), None, OP.is_equal)
-    ts(ch("on"), A("m32", 0, 128), col(4), None, OP.is_equal)
-    ts(ch("lt"), row128, col(0), None, OP.is_ge)
-    tt(ch("lt"), ch("lt"), ch("on"), OP.mult)
-    ts(ch("ones"), row128, 0.0, 1.0, OP.mult, OP.add)
+    ts(A("pc", 0, 8), A("dum", 0, 8), 16.0, float(8 - 16 * V), OP.mult, OP.add)
+    act(A("u1f", 0, 144), cb("u1"), AF.Copy)
+    ts(cb("on"), A("m32", 0, 128), col(4), None, OP.is_equal)
+    ts(cb("lt"), row128, col(0), None, OP.is_ge)
+    tt(cb("lt"), cb("lt"), cb("on"), OP.mult)
+    act(cb("ones"), row128, scale=0.0, bias=1.0)
+    act(cb("c13"), A("row", 0, 16), scale=0.0, bias=1344.0)
+    if NSB < 16:
+        act(cb("ih"), cb("i1"), AF.Copy, scale=0.5)
+        act(cb("u64"), cb("u1"), AF.Copy, scale=64.0)
+        act(cb("um32"), cb("u1"), AF.Copy, scale=-32.0)
+        ts(cb("bv16"), j128, float(NSB), -16.0, OP.is_ge, OP.mult)
+        tt(cb("bv16"), cb("bv16"), cb("bo1"), OP.mult)
+        act(cb("bv32"), cb("bv16"), AF.Copy, scale=2.0)
+    act(cb("m512"), row128, scale=0.0, bias=-512.0)
+    act(cb("c75"), A("row", 0, 2), scale=0.0, bias=-7.5)
+    ts(A("col", 40, 56), A("jr", 0, 16), col(1), None, OP.is_equal)
     for q in range(16):
-        ts(col(40 + q), col(1), float(q), None, OP.is_equal)
-    for q in range(16):
-        ts(ch("rq", 128 * q, 128), ch("bo1"), col(40 + q), None, OP.mult)
-    for nm in ("tab1", "tab2", "tab3"):
-        fill(A(nm, V, REM), 0.0)
-    fill(A("nb", V, REM), 0)
+        act(cb("rq", 128 * q, 128), cb("bo1"), AF.Copy, scale=col(40 + q))
+    for c in range(NC):
+        ts(A("wfl1", 16 * c, 16 * c + 8), cw("v0w", c), -1344.0, None, OP.add)
+    act(A("wrp1", 0, L), A("v2", 0, L), scale=0.5, bias=-1344.5)
     cp(col(18), A("thi", 0, 1))
-    ts(col(19), col(18), 32.0, None, OP.mult)
-    tt(col(22), col(19), col(6), OP.add)
+    ts(col(22), col(18), 32.0, col(6), OP.mult, OP.add)
     ts(col(23), col(22), -BIG, BIG, OP.mult, OP.add)
-    ts(ch("im"), row128, col(0), -1.0, OP.is_equal, OP.mult)
-    act(cb("ih"), cb("i1"), AF.Copy, scale=0.5)
+    act(cb("i1k"), cb("i1"), AF.Copy, scale=1024.0)
     act(cb("imh"), cb("i1"), AF.Copy, scale=-0.5)
     act(cb("i256"), cb("i1"), AF.Copy, scale=-256.0)
     act(cb("boh"), cb("bo1"), AF.Copy, scale=0.5)
     ts(cb("tri"), A("jr", 0, 256), col(1), 32768.0, OP.is_le, OP.mult)
-    remote(prv, A("tab0", 0, H), A("rem0", 0, H), nxt, "push0", "pl0", 2 * 128 * H)
+    def pushes(t):
+        for x, lo, hi, to in (("a", 1024, 2048, 0), ("b", 0, 1026, 1024)):
+            remote(prv, A("tab%d" % t, lo, hi), A("rem%d" % t, to, to + hi - lo), nxt, "push%s%d" % (x, t), "pl%s%d" % (x, t),
+                   256 * (hi - lo))
 
-    def l2wrap(out, src, first=None):
+    pushes(0)
+
+    def l2p(out, src):
         (nm, lo, hi), (sn, slo, shi) = out, src
-        if first is not None:
-            mm(A(nm, lo, hi), first[0], first[1], True, False)
-        for c2 in range(2):
-            for g2 in range(2):
-                mm(A(nm, lo + c2, hi, 2), ch("sl", 128 * (2 * g2 + c2), 128), A(sn, slo + g2, shi, 2),
-                   first is None and g2 == 0, g2 == 1 and (first is None or c2 == 1))
+        return [(cb("sl", 128 * (2 * g2 + c2), 128), A(sn, slo + g2, shi, 2), A(nm, lo + c2, hi, 2))
+                for c2 in range(2) for g2 in range(2)]
 
-    def l2direct(c, o, nm, mats):
+    def l2wrap(out, src):
+        prs = l2p(out, src)
+        group(None, prs[:2])
+        group(None, prs[2:])
+
+    def l2direct(c, o, nm):
         a = NL * c
-        big = "ch" if mats is ch else "cb"
-        lo = (CHN if mats is ch else CBN)["bo1"][0]
+        lo = CBN["bo1"][0]
         bank = "ps%d" % (4 + c)
         for pa in range(4):
             for ib in range(4):
                 out = ([(bank, 0, 1)], T[bank][32 * pa:32 * pa + 32, o + 2 * ib:o + 2 * ib + 2], 2)
-                mm(out, A(nm, a + 32 * ib, a + 32 * ib + 32), A(big, lo + 32 * pa, lo + 32 * pa + 32, 16), True, True)
+                mm(out, A(nm, a + 32 * ib, a + 32 * ib + 32), A("cb", lo + 32 * pa, lo + 32 * pa + 32, 16), True, True)
 
     def clean_q(t, c, nm):
         x = ck(nm, c)
@@ -366,13 +372,12 @@ def rank_program(g, core, T, topo):
         z = ck(zbuf(t), c)
         m = AC(c, 128, 256)
         mm(SM(c, 0, 128), cb("bo1" if t == 0 else "boh"), z, True, True)
-        mm(KA(c, 256, 384), cb("i1" if t == 0 else "ih"), z, True, True)
-        act(ck("zs", c), KA(c, 256, 384), bias=-0.5)
-        ts(ck("yi", c), SM(c, 0, 128), col(36 + t), None, OP.add)
+        act(ck("zs", c), z, scale=1.0 if t == 0 else 0.5, bias=-0.5)
+        ts(ck("yi", c), SM(c, 0, 128), col(36), float(t), OP.add, OP.add)
         ts(ck("yj", c), ck("yi", c), 15, None, OP.bitwise_and)
         ts(m, ck("yj", c), 0.0, None, OP.is_equal)
         tt(ck("nm", c), ck("bv", c), m, OP.mult)
-        group(SM(c, 128, 136), [(U("u1", q, True), A("nm", a + q, a + NL, 16)) for q in range(16)])
+        group(SM(c, 128, 136), [(U("u1", q), A("nm", a + q, a + NL, 16)) for q in range(16)])
         ts(cw("nl", c), SM(c, 128, 136), 1344.0, None, OP.add)
         cp(ck("cd", c), ind(A("nb", 0, V), cw("nl", c)))
         kc = "kc%d" % c
@@ -380,9 +385,9 @@ def rank_program(g, core, T, topo):
             act(A(kc, 2048 // SUBK * s, 2048 // SUBK * (s + 1)),
                 ind(tabw(t), A("cd", a + 128 // SUBK * s, a + 128 // SUBK * (s + 1))))
         cp(ck("kn", c), ind(tabw(t), cw("nl", c)))
-        l2direct(c, 160, "nm", ch)
+        l2direct(c, 160, "nm")
         tt(ck("e0", c), ck("kn", c), KA(c, 0, 128), OP.is_equal)
-        l2direct(c, 168, "e0", cb)
+        l2direct(c, 168, "e0")
         ts(ck("cdh", c), ck("cd", c), -1344.0, None, OP.add)
         group(KA(c, 128, 256), clean_q(t, c, "kn"))
         if NSV:
@@ -406,8 +411,10 @@ def rank_program(g, core, T, topo):
                     mm(o, cb("i1"), A(kc, 12 - 4 * b + j, 2048, 16), True, False)
                     mm(o, cb("im"), ck(neg, c), False, True)
                 act(A(db, hi - 512, hi), DB(bk, 0, 512), AF.Copy)
-                ts(A(e, hi - 512, hi), A(db, hi - 512, hi), 0.0, None, OP.is_equal)
-            mm(out, ch("i1"), ck("cdh", c), True, False)
+                if b % EQB == EQB - 1:
+                    w = 512 * EQB
+                    ts(A(e, hi - 512, hi - 512 + w), A(db, hi - 512, hi - 512 + w), 0.0, None, OP.is_equal)
+            mm(out, cb("i1"), ck("cdh", c), True, False)
             mm(out, cb("i1"), cb("kb"), False, False)
             for k in range(16):
                 ek = A(e, 128 * k, 128 * k + 128)
@@ -415,7 +422,7 @@ def rank_program(g, core, T, topo):
                     tt(ek, A(kc, k, 2048, 16), KA(c, lo, lo + 128), OP.is_equal)
                 mm(out, U("u17", k), ek, False, k == 15)
             if lo == 0:
-                act(ck("av", c), out, AF.Copy)
+                cp(ck("av", c), out)
         act(ck("kvr", c), KA(c, 0, 128), AF.Relu)
         tt(ck("val", c), ck("av", c), AC(c, 0, 128), OP.min)
         tr(ck("vt", c), ck("val", c))
@@ -429,8 +436,7 @@ def rank_program(g, core, T, topo):
         l2wrap((sm, 136, 144), ("w16", 8 * c, 8 * c + 8))
         l2wrap((sm, 144, 152), ("fl", 8 * c, 8 * c + 8))
         ts(cw("wl%d" % t, c), SM(c, 136, 144), 1344.0, None, OP.add)
-        cp(A("wfl", 16 * c, 16 * c + 16), SM(c, 136, 152))
-        ts(cw("wr%d" % t, c), SM(c, 136, 144), 1344.0, None, OP.add)
+        cp(A("wfl%d" % (t & 1), 16 * c, 16 * c + 16), SM(c, 136, 152))
 
     def stage_w(t, c):
         a = NL * c
@@ -447,7 +453,7 @@ def rank_program(g, core, T, topo):
         kw = SM(c, 0, 128)
         group(kw, prs)
         tt(ck("pi", c), ck("v2", c), kw, OP.mult)
-        ts(ck("pj", c), ck("pi", c), col(8 + t), None, OP.add)
+        ts(ck("pj", c), ck("pi", c), col(8), float(4 * t), OP.add, OP.add)
         ts(ck("pk", c), ck("pj", c), 2, PL - 1, OP.arith_shift_right, OP.bitwise_and)
         cp(ck("pl", c), ck("pk", c))
         for s in range(SUBX):
@@ -457,71 +463,71 @@ def rank_program(g, core, T, topo):
         act(ck("kwc", c), kw, AF.Copy)
         act(ck("hb", c), ck("kwc", c), AF.Relu, scale=-BIG, bias=col(16))
         for q in range(16):
-            mm(SM(c, 256 + q, 512, 16), ch("rq", 128 * q, 128), A("wfl", 16 * c, 16 * c + 16), True, True)
+            mm(SM(c, 256 + q, 512, 16), cb("rq", 128 * q, 128), A("wfl%d" % (t & 1), 16 * c, 16 * c + 16), True, True)
         act(ck("flr", c), SM(c, 384, 512), scale=-512.0)
-        act(ck("nfr", c), SM(c, 384, 512), scale=512.0, bias=-512.0)
         if t < NR - 1:
             act(ck("v2", c), SM(c, 256, 384), scale=2.0, bias=2689.0)
-            vr = ck("vrh%d" % (t & 1), c)
-            cp(vr, SM(c, 256, 384))
+            vr = ck("wrp%d" % (t & 1), c)
+            act(vr, SM(c, 256, 384), AF.Copy)
             tt(ck("wm", c), vr, AC(c, 128, 256), OP.mult)
 
     def stage_full(t):
-        group(F1(0, 16), [(ch("lt"), fu("fl"))]
-              + [(ch("on"), A("fl", 0, 16 - 2 * d), F1(2 * d, 16)) for d in range(1, 8)])
-        mm(F1(16, 32), ch("ones"), fu("fl"), True, True)
-        ts(fu("ns0"), F1(0, 16), 64.5, None, OP.is_gt)
-        tt(fu("ns"), fu("ns0"), fu("fl"), OP.mult)
-        ts(fu("dr"), fu("tot"), 2.2e6 - 2.5 * S17, None, OP.is_gt)
-        tt(fu("iah"), fu("ns"), fu("dr"), OP.add)
-        l2wrap(("ps1", 432, 448), ("iah", 0, 16))
+        ts(fu("dr"), fu("tot"), 2.2e6 - 2.5 * S17, 2048.0, OP.is_gt, OP.mult)
+        group(F1(0, 16), [(cb("lt"), fu("fl"))]
+              + [(cb("on"), A("fl", 0, 16 - 2 * d), F1(2 * d, 16)) for d in range(1, 8)]
+              + [(cb("i1k"), fu("fl")), (cb("i1"), fu("dr"))])
+        ts(fu("iah"), F1(0, 16), 1024.0 + CAP + 0.5, 16384.0, OP.is_gt, OP.mult)
+        vprev = "wfl%d" % ((t + 1) & 1)
+
+        def node(lo):
+            return [(cb("i1"), cb("c13"))] + [(cb("i1"), A(vprev, 16 * c, 16 * c + 8), F1(lo + 8 * c, lo + 8 * c + 8))
+                                              for c in range(NC)] + l2p(("ps1", 384 + lo, 400 + lo), ("iah", 0, 16))
         group(F1(64, 80), [(A("u1f", 15 - q, 143 - q), A("pz", q, L, 16)) for q in range(16)])
-        cp(fu("iaw"), F1(48, 64))
         zs = 1.0 if t == 0 else 2.0
         big = 1.5 * 2 ** 34 * zs
         ts(fu("hH"), F1(64, 80), big, -big, OP.add, OP.add)
         tt(fu("h2"), F1(64, 80), fu("hH"), OP.subtract)
-        ts(fu("hx"), fu("h2"), 0.0, H * zs, OP.is_lt, OP.mult)
-        tt(fu("hy"), fu("h2"), fu("hx"), OP.add)
-        ts(fu("sl2"), fu("hy"), 1.0 / zs, None, OP.mult)
+        ts(fu("sl2"), fu("h2"), 1.0 / zs, 1024.0, OP.mult, OP.add)
         tab = "tab%d" % (t + 1)
-        act(A("src", 0, L), ind(A("rem%d" % t, 0, H), fu("sl2")))
+        act(A("src", 0, L), ind(A("rem%d" % t, 0, H + 1), fu("sl2")))
         if t < NR - 1:
-            red(A("fs", 0, 1), F1(16, 32), OP.add)
-            ts(A("fs", 1, 2), A("fs", 0, 1), -7.5, None, OP.add)
+            ones = [(cb("ones"), A("fl", j, j + 1)) for j in range(16)]
+            group(F1(16, 17), ones)
+            group(F1(17, 18), ones + [(cb("i1"), cb("c75", 0, 1))])
             b27 = 1.5 * 2 ** 27
-            ts(A("fs", 2, 3), A("fs", 1, 2), b27, -b27, OP.add, OP.add)
-            tt(A("fs", 3, 4), A("fs", 0, 1), A("fs", 2, 3), OP.subtract)
-        vw = fu("v0w") if t == 0 else fu("wr%d" % (t - 1))
-        tt(fu("vmd"), vw, fu("dum"), OP.subtract)
+            ts(A("fs", 2, 3), F1(17, 18), b27, -b27, OP.add, OP.add)
+            tt(A("fs", 3, 4), F1(16, 17), A("fs", 2, 3), OP.subtract)
         if t > 0:
-            ts(fu("va"), fu("iaw"), 16384.0, -1344.0, OP.mult, OP.add)
-            tt(fu("vb"), fu("va"), vw, OP.add)
-            cp(fu("vah"), fu("vb"))
-            vr = "vrh%d" % ((t - 1) & 1)
+            group(F1(48, 64), node(48))
+            act(fu("vb"), F1(48, 64), bias=-1344.0)
+            ts(fu("vah"), F1(48, 64), -1344.0, None, OP.add)
+            vr = "wrp%d" % ((t - 1) & 1)
             group(KA(0, 0, 256), [(cb("i1"), cb("tri"))]
-                  + [(ch("i1"), fu("vah"), KA(0, q, 256, 16)) for q in range(16)])
+                  + [(cb("i1"), fu("vah"), KA(0, q, 256, 16)) for q in range(16)])
             o = 0
             prs = [(cb("bo1"), A("ed", 0, L))]
             for c1 in range(15):
                 n = L - 16 * (c1 + 1)
-                ts(A("e3", o, o + n), A(vr, L - n, L), A("vb", c1, c1 + 1), None, OP.is_equal)
+                if c1 < E3S:
+                    act(A("e3", o, o + n), A(vr, L - n, L), scale=-1.0, bias=A("vb", c1, c1 + 1))
+                    oe = o + n
+                else:
+                    ts(A("e3", o, o + n), A(vr, L - n, L), A("vb", c1, c1 + 1), None, OP.is_equal)
                 prs.append((cb("bo1"), A("e3", o, o + n), KA(1, 256 - n, 256)))
                 o += n
             tt(A("ed", 0, L), A(vr, 0, L), KA(0, 0, 256), OP.is_equal)
+            if E3S:
+                ts(A("e3", 0, oe), A("e3", 0, oe), 0.0, None, OP.is_equal)
             group(KA(1, 0, 256), prs)
             act(A("cnb", 0, L), KA(1, 0, 256), AF.Copy)
-            group(F1(80, 96), [(U("u1", q), A("cnb", q, L, 16)) for q in range(16)])
-            tt(fu("nw"), fu("iaw"), F1(80, 96), OP.add)
-            ts(fu("wrt"), fu("nw"), 0.5, None, OP.is_lt)
+            group(F1(80, 96), node(80) + [(U("u17", q), A("cnb", q, L, 16)) for q in range(16)])
         else:
-            ts(fu("wrt"), fu("iaw"), 0.5, None, OP.is_lt)
-        tt(fu("sx"), fu("wrt"), fu("vmd"), OP.mult)
-        tt(fu("sy"), fu("sx"), fu("dum"), OP.add)
+            group(F1(80, 96), node(80))
+        tt(fu("sy"), fu("dum"), F1(80, 96), OP.min)
         cp(fu("sl"), fu("sy"))
         for c in range(NC):
             o = SM(c, 256, 384)
-            for x, fm in (("kwc", "flr"), ("src", "nfr")):
+            for x in ("kwc", "src"):
                 mm(o, cb("i1"), ck(x, c), True, False)
                 if x == "src" and t >= 1:
                     ts(ck("sa", c), ck("src", c), A("rc%d" % (t - 1), 0, 1), A("rc%d" % (t - 1), 0, 1), OP.is_equal, OP.mult)
@@ -529,15 +535,17 @@ def rank_program(g, core, T, topo):
                 if x == "src" and t >= 2:
                     ts(ck("sb", c), ck("src", c), A("ra0", 0, 1), A("ra0", 0, 1), OP.is_equal, OP.mult)
                     mm(o, cb("im"), ck("sb", c), False, False)
-                mm(o, cb("i1"), ck(fm, c), False, False)
+                if x == "src":
+                    mm(o, cb("i1"), cb("m512"), False, False)
+                mm(o, cb("i1" if x == "kwc" else "im"), ck("flr", c), False, False)
                 mm(o, cb("i256"), ck("kvr", c), False, True)
                 tt(ck("f1" if x == "kwc" else "fi", c), ck("kvr" if x == "kwc" else "f1", c), o, OP.max)
         cp(ind(A(tab, 0, REM), fu("sl")), A("fi", 0, L))
         if t < NR - 1:
-            group(KA(0, 256, 512), [(ch("i1"), A("bv", 0, L)), (ch("im"), A("nm", 0, L)), (ch("i1"), A("wm", 0, L))])
+            group(KA(0, 256, 512), [(cb("i1"), A("bv", 0, L)), (cb("im"), A("nm", 0, L)), (cb("i1"), A("wm", 0, L))])
             act(A("bn", 0, L), KA(0, 256, 512), bias=1344.0)
             cp(ind(A("nb", 0, REM), fu("sl")), A("bn", 0, L))
-            remote(prv, A(tab, 0, H), A("rem%d" % (t + 1), 0, H), nxt, "push%d" % (t + 1), "pl%d" % (t + 1), 2 * 128 * H)
+            pushes(t + 1)
             dma("y", A("tab%d" % (t + 2), 0, V), A(tab, 0, V), 2 * 128 * V)
 
     def stage_d(t, c):
@@ -546,7 +554,10 @@ def rank_program(g, core, T, topo):
         out = AC(c, 256, 384)
         xc = "xc%d" % c
         mm(out, cb("i1"), cb("pt"), True, False)
-        for b in range(4):
+        if NSB < 16:
+            mm(KA(c, 256, 384), cb("i1" if t == 0 else "ih"), z, True, True)
+            mm(out, cb("bv32" if t == 0 else "bv16"), z, False, False)
+        for b in range(NSB // 4):
             bk = nb_[0] % 2
             nb_[0] += 1
             for j in range(4):
@@ -554,15 +565,20 @@ def rank_program(g, core, T, topo):
                 mm(o, cb("i1"), A(xc, 4 * b + j, 2048, 16), True, False)
                 mm(o, cb("im" if t == 0 else "imh"), z, False, True)
             act(A("mx%d" % c, 512 * b, 512 * b + 512), DB(bk, 0, 512), AF.Abs)
-        for p in range(16):
-            mm(out, U("u32", p), A("mx%d" % c, 128 * p, 128 * p + 128), False, p == 15)
+        for p in range(15, -1, -1):
+            mxp = A("mx%d" % c, 128 * p, 128 * p + 128)
+            if p >= NSB:
+                x = A(xc, p, 2048, 16)
+                mm(out, U("um32", p), x, False, False)
+                tt(mxp, x, KA(c, 256, 384), OP.max)
+            mm(out, U("u32" if p < NSB else "u64", p), mxp, False, p == 0)
         tr(ck("dt", c), out)
         scan(ck("ds", c), A("mnm", 0, 128), ck("dt", c), OP.max, OP.min)
         b28 = 1.5 * 2 ** 28
         last = A("ds", a + 15, a + NL, 16)
         ts(cw("pH", c), last, b28, -b28, OP.add, OP.add)
         tt(cw("p16", c), last, cw("pH", c), OP.subtract)
-        l2wrap(("ps%d" % (4 + c), 152, 160), ("p16", 8 * c, 8 * c + 8), (ch("i1"), ch("pc")))
+        group(SM(c, 152, 160), [(cb("i1"), A("pc", 0, 8))] + l2p(("ps%d" % (4 + c), 152, 160), ("p16", 8 * c, 8 * c + 8)))
         cp(cw("pw", c), SM(c, 152, 160))
         tt(ck("sz", c), ind(A(xc, 0, 2048), cw("pw", c)), ck("zs", c), OP.add)
         b24 = 1.5 * 2 ** 24
@@ -624,19 +640,23 @@ def rank_program(g, core, T, topo):
             for q, lo, hi in (("y", 0, 768), ("s", 768, 1536), ("y", 1536, 2304), ("s", 2304, V)):
                 dma(q, hbm("yk", lo, hi), A("fin", lo, hi), 256 * (hi - lo))
 
+    stages = {"v": stage_v, "n": stage_n, "c": stage_cmp, "w": stage_w, "d": stage_d}
+
     def st(f, t, c):
-        bon[0] = BON * (1 - c)
-        f(t, c)
+        bon[0] = BT[f][c]
+        stages[f](t, c)
         bon[0] = 0.0
 
     for t in range(NR):
         for c in range(NC):
-            st(stage_v, t, c)
-            st(stage_n, t, c)
+            st("v", t, c)
+            st("n", t, c)
         for c in range(NC):
-            st(stage_cmp, t, c)
-            st(stage_w, t, c)
+            st("c", t, c)
+            st("w", t, c)
+        bon[0] = BT["f"][0]
         stage_full(t)
+        bon[0] = 0.0
         if t == 1:
             clean("tab3", "tab2", "clb", (A("rb0", 0, 1), A("rb0", 2, 3)))
         if t == 2:
@@ -645,7 +665,7 @@ def rank_program(g, core, T, topo):
                 ts(A("clb", lo, hi), A("tab3", lo, hi), A("rb1", 0, 1), A("rb1", 2, 3), OP.is_equal, OP.mult)
             bon[0] = 0.0
         for c in range(NC):
-            st(stage_d, t, c)
+            st("d", t, c)
         if t < NR - 1:
             ts(A("fs", 5 + t, 6 + t), A("fs", 3, 4), -32.0 * BIG, col(23), OP.mult, OP.add)
         stage_rv(t)

from concourse.mybir import AluOpType, AxisListType, ActivationFunctionType

OP = AluOpType
AF = ActivationFunctionType
V, PL, L, NR, H = 2688, 4096, 256, 3, 2048
REM = V + L
NC, NL = 2, 128
S17 = float(2 ** 17)
BIG = float(2 ** 20)
CYC, PEC, VF, SF, WK, GA, SCA = 0.83, 0.42, 80.0, 100.0, 60.0, 1.5, 3.0
CLB = 15000.0
BT = {"v": (0.0, 0.0), "n": (1700.0, 0.0), "c": (2000.0, 0.0), "w": (8800.0, 600.0), "d": (3800.0, 700.0), "f": (0.0,)}
CAP = 64
NSB, E3S = 16, 0
NSV, NSN, EQB, SUBK, SUBX = 0, 16, 1, 2, 2
CBN = {}
ALIAS = {}
SCRATCH = {}


def _lay(d, names):
    o = 0
    for nm, w in names:
        d[nm] = (o, o + w)
        o += w
    return o


def _small(big, dtype, names):
    o = 0
    for nm in names:
        ALIAS[nm] = (big, o)
        o += 32 if nm[:3] == "wfl" else 16
    SCRATCH[big] = ("sbuf", [128, o], dtype)


def _bufs(dtype, width, names):
    for nm in names:
        SCRATCH[nm] = ("sbuf", [128, width], dtype)


CBW = _lay(CBN, [("u17", 144), ("u32", 144), ("u1", 144), ("bo1", 128), ("boh", 128), ("i1", 128),
                 ("im", 128), ("imh", 128), ("i256", 128), ("i1k", 128), ("kb", 128), ("pt", 128), ("io", 256), ("tri", 256),
                 ("on", 128), ("lt", 128), ("ones", 128), ("sl", 512), ("rq", 2048), ("c13", 16), ("c75", 2),
                 ("m512", 128), ("ih", 128), ("u64", 144), ("um32", 144), ("bv16", 128), ("bv32", 128)])
_bufs("bfloat16", REM, ("tab0", "tab1", "tab2", "tab3"))
_bufs("bfloat16", H + 16, ("rem0", "rem1", "rem2"))
_bufs("bfloat16", H, ("kc0", "kc1", "e10", "e11", "e20", "e21", "xc0", "xc1", "mx0", "mx1", "da0",
                      "da1", "db0", "db1"))
_bufs("bfloat16", V, ("cln", "clb", "fin"))
_bufs("bfloat16", L, ("zi", "zb", "kv", "kn", "q0", "qa", "qb", "e0", "kw", "kwc", "src", "sa", "sb", "f1", "hb", "ug",
                      "flr", "nfr", "kvr", "knp", "kvp", "fi", "ed", "cnb"))
_bufs("float16", L, ("bv", "nm", "cdh", "wm"))
_bufs("float16", 8, ("pc",))
_bufs("float32", L, ("wrp0", "wrp1", "row", "jr", "tmpc", "av", "val", "vt", "sc", "v2", "pz", "dt", "ds", "xm", "sz", "zs", "bn", "yzf"))
_bufs("float32", 128, ("m32", "mxm", "mnm"))
_bufs("int32", L, ("yi", "yj", "pi", "pj", "pk"))
_bufs("uint16", L, ("cd", "pl"))
_bufs("float32", 4, ("ra0", "ra1", "ra2", "rb0", "rb1", "rc0", "rc1"))
_bufs("float32", 8, ("fs", "rr"))
_bufs("int32", 8, ("ipc",))
_small("smu", "uint16", ("nl", "pw", "sl2", "sl", "wl0", "wl1", "wl2"))
_small("sm32", "float32", ("dk", "nk16", "tot", "th", "hH", "h2", "vb", "sy", "pH", "dum", "v0w"))
_small("sm16", "float16", ("w16", "fl", "dr", "iah", "vah", "p16", "wfl0", "wfl1"))
SCRATCH["nb"] = ("sbuf", [128, REM], "int32")
SCRATCH["X"] = ("sbuf", [128, PL], "bfloat16")
SCRATCH["thi"] = ("sbuf", [128, 1], "int32")
SCRATCH["cb"] = ("sbuf", [128, CBW], "bfloat16")
SCRATCH["u1f"] = ("sbuf", [128, 144], "float32")
SCRATCH["col"] = ("sbuf", [128, 64], "float32")
SCRATCH["e3"] = ("sbuf", [128, 1920], "bfloat16")
for _b in range(8):
    SCRATCH["ps%d" % _b] = ("psum", [128, 512], "float32")
SEMAPHORES = ["qv", "qs", "qp", "qg"] + ["d%d" % i for i in range(40)] \
    + [a + str(i) for a in ("pusha", "pushb", "pla", "plb", "rvs", "rvl", "rws", "rwl") for i in range(3)]


def rank_program(g, core, T, topo):
    rank = T.rank_of(core)
    if rank is None:
        return
    nranks = len(T.cores)
    nxt, prv = T.cores[(rank + 1) % nranks], T.cores[(rank - 1) % nranks]
    ops, hist, ndma, bon, nb_ = [], {}, [0], [0.0], [0]

    def A(name, lo, hi, st=1):
        if name in ALIAS:
            name, o = ALIAS[name]
            lo, hi = lo + o, hi + o
        ap = T[name][:, lo:hi] if st == 1 else T[name][:, lo:hi:st]
        return ([(name, lo, hi)], ap, (hi - lo + st - 1) // st)

    def cb(nm, lo=0, w=None):
        o, e = CBN[nm]
        return A("cb", o + lo, e if w is None else o + lo + w)

    def U(nm, q):
        return cb(nm, 15 - q, 128)

    def ind(win, lst):
        return (win[0] + lst[0], win[1].indirect(lst[1]), 16 * lst[2], 1)

    def op(q, dur, rd, wr, call, sem=None, val=1, lat=0.0):
        i = len(ops)
        deps = {}
        for regs, w in ((rd, 0), (wr, 1)):
            for nm, lo, hi in regs:
                if nm[:2] == "ps":
                    for q2, j in hist.get(nm, {}).items():
                        if j != i:
                            deps[j] = deps.get(j, False) or q2 != q or q != "p"
                else:
                    for j, l2, h2, w2 in hist.get(nm, []):
                        if j != i and l2 < hi and lo < h2 and (w or w2):
                            deps[j] = True
        for regs, w in ((rd, 0), (wr, 1)):
            for nm, lo, hi in regs:
                if nm[:2] == "ps":
                    hist.setdefault(nm, {})[q] = i
                else:
                    a = hist.setdefault(nm, [])
                    if w:
                        a[:] = [e for e in a if e[0] == i or not (lo <= e[1] and e[2] <= hi)]
                    a.append((i, lo, hi, w))
        ops.append({"q": q, "dur": dur, "deps": deps, "call": call, "sem": sem, "val": val, "lat": lat, "bon": bon[0]})
        return i

    def vdur(n, f):
        return max(64.0, n * f) * CYC + VF

    def two(*xs):
        return all(SCRATCH[x[0][0][0]][2] in ("bfloat16", "float16", "uint16") for x in xs)

    def sc_(x):
        return (x[1], x[0]) if isinstance(x, tuple) else (x, [])

    def ts(out, a, s1, s2, o0, o1=None):
        x1, r1 = sc_(s1)
        x2, r2 = sc_(s2)
        f = GA if len(a) > 3 else (0.5 if two(out, a) else 1.0)
        if o1 is None:
            def call():
                return g.vector.tensor_scalar(out[1], a[1], x1, None, o0)
        else:
            def call():
                return g.vector.tensor_scalar(out[1], a[1], x1, x2, o0, o1)
        return op("v", vdur(a[2], f), a[0] + r1 + r2, out[0], call)

    def tt(out, a, b, o):
        ps = a[0][0][0][:2] == "ps" or b[0][0][0][:2] == "ps"
        return op("v", vdur(b[2], GA if len(a) > 3 else 1.0 if ps else 2.0), a[0] + b[0], out[0],
                  lambda: g.vector.tensor_tensor(out[1], a[1], b[1], o))

    def cp(out, a):
        f = SCA if len(out) > 3 else GA if len(a) > 3 else (0.5 if two(out, a) else 1.0)
        wr = out[0][:1] if len(out) > 3 else out[0]
        rd = a[0] + (out[0][1:] if len(out) > 3 else [])
        return op("v", vdur(a[2], f), rd, wr, lambda: g.vector.tensor_copy(out[1], a[1]))

    def red(out, a, o):
        return op("v", vdur(a[2], 1.0), a[0], out[0], lambda: g.vector.tensor_reduce(out[1], a[1], AxisListType.X, o))

    def scan(out, d0, d1, o0, o1):
        return op("v", vdur(d1[2], 1.0), d0[0] + d1[0], out[0],
                  lambda: g.vector.tensor_tensor_scan(out[1], d0[1], d1[1], 0.0, o0, o1))

    def tr(out, a):
        return op("v", vdur(a[2], 1.0), a[0], out[0], lambda: g.vector.transpose(out[1], a[1]))

    def fill(out, c):
        return op("v", vdur(out[2], 0.5), [], out[0], lambda: g.vector.memset(out[1], c))

    def act(out, a, func=None, scale=1.0, bias=0.0):
        x, r = sc_(bias)
        y, r2 = sc_(scale)
        fn = AF.Identity if func is None else func
        return op("s", a[2] * (GA if len(a) > 3 else 1.0) * CYC + SF, a[0] + r + r2, out[0],
                  lambda: g.scalar.activation(out[1], a[1], fn, bias=x, scale=y))

    def mm(out, lhsT, rhs, start, stop):
        f = 4 if SCRATCH[rhs[0][0][0]][2] == "float32" else 1
        return op("p", max(min(64.0, lhsT[2]), rhs[2]) * f * PEC, lhsT[0] + rhs[0], out[0],
                  lambda: g.tensor.matmul(out[1], lhsT[1], rhs[1], start, stop))

    def group(out, pairs):
        for i, pr in enumerate(pairs):
            mm(pr[2] if len(pr) > 2 else out, pr[0], pr[1], i == 0, i == len(pairs) - 1)

    def iota(out, pat, base, mul):
        if SCRATCH[out[0][0][0]][2] != "int32":
            def call():
                return g.iota(out[1], pat, base, mul, allow_small_or_imprecise_dtypes=True)
        else:
            def call():
                return g.iota(out[1], pat, base, mul)
        return op("g", 130 + 2 * out[2] * CYC, [], out[0], call)

    def dma(q, out, a, nbytes, add=False, after=()):
        s = "d%d" % ndma[0]
        ndma[0] += 1
        eng = {"y": g.sync, "s": g.scalar, "g": g}[q]
        if add:
            def call():
                return eng.dma_start(out[1], a[1], accum_op=OP.add)
        else:
            def call():
                return eng.dma_start(out[1], a[1])
        return op(q, 1000 if q == "g" else 60, a[0] + (out[0] if add else []) + [(x, 0, 1) for x in after], out[0], call, sem=s, val=16,
                  lat=1900 + nbytes / 180.0)

    def hbm(name, lo, hi):
        return ([("hbm_" + name, lo, hi)], T[name][:, lo:hi], hi - lo)

    def remote(dst, src, out, frm, rsem, lsem, nbytes):
        rid, pid, _se = topo.addr(dst)
        msk = topo.mask(core, dst)
        ne = len(topo.engines(core, dst))
        op("g", 1000, src[0], [], lambda: g.remote_dma(out[1], src[1], T.sem[rsem], T.sem[lsem], pid, rid, msk),
           sem=lsem, val=ne, lat=2000 + nbytes / 60.0)
        ops[-1]["remote"] = True
        op("ext", 0, [], out[0], None, sem=rsem, val=len(topo.engines(frm, core)))
        ops[-1]["after"] = len(ops) - 2

    def KA(c, lo, hi, st=1): return A("ps%d" % c, lo, hi, st)
    def AC(c, lo, hi): return A("ps%d" % (2 + c), lo, hi)
    def SM(c, lo, hi, st=1): return A("ps%d" % (4 + c), lo, hi, st)
    def DB(b, lo, hi): return A("ps%d" % (6 + b), lo, hi)
    def F1(lo, hi): return A("ps1", 384 + lo, 384 + hi)
    def col(i): return A("col", i, i + 1)
    def ck(name, c): return A(name, NL * c, NL * c + NL)
    def cw(name, c): return A(name, 8 * c, 8 * c + 8)
    def fu(name): return A(name, 0, 16)
    def tabw(t): return A("tab%d" % t, 0, V)
    def zbuf(t): return "zi" if t == 0 else "zb"

    dma("s", A("zi", 0, L), hbm("z0", 0, L), 2 * 128 * L)
    dma("y", A("nb", 0, V), hbm("nbr", 0, V), 4 * 128 * V)
    dma("s", A("tab0", 0, V), hbm("ring", 0, V), 2 * 128 * V)
    dma("s", A("thi", 0, 1), hbm("thr", 0, 1), 512)
    dma("y", A("X", 0, PL), hbm("mat", 0, PL), 2 * 128 * PL, after=("nb", "tab0"))
    dma("y", A("tab1", 0, V), hbm("ring", 0, V), 2 * 128 * V, after=("X",))

    iota(A("ipc", 0, 1), [[0, 1]], 0, 1)
    iota(A("row", 0, 256), [[1, 256]], 0, 0)
    iota(A("jr", 0, 256), [[0, 16], [1, 16]], 0, 0)
    iota(A("m32", 0, 128), [[32, 4], [0, 32]], 0, 0)
    iota(fu("dum"), [[16, 16]], V, 1)
    iota(fu("v0w"), [[160, 16]], 0, 10)
    iota(A("v2", 0, 256), [[20, 256]], 1, 0)
    ip = A("ipc", 0, 1)
    ts(A("ipc", 1, 2), ip, 15, None, OP.bitwise_and)
    ts(A("ipc", 2, 3), ip, 96, None, OP.bitwise_and)
    ts(A("ipc", 3, 4), ip, 4, 1, OP.logical_shift_right, OP.bitwise_and)
    cp(A("col", 0, 2), A("ipc", 0, 2))
    cp(A("col", 4, 6), A("ipc", 2, 4))
    tt(col(2), col(0), col(1), OP.subtract)
    ts(col(3), col(2), 15.0, None, OP.add)
    ts(col(36), col(1), -1.0, 16.0, OP.mult, OP.add)
    ts(col(8), col(1), 3244.0, None, OP.mult)
    row128 = A("row", 0, 128)
    row144 = A("row", 0, 144)
    j128 = A("jr", 0, 128)
    tt(A("tmpc", 0, 256), A("row", 0, 256), A("jr", 0, 256), OP.subtract)
    m16 = A("tmpc", 0, 128)
    ts(cb("i1"), row128, col(0), None, OP.is_equal)
    act(cb("im"), cb("i1"), AF.Copy, scale=-1.0)
    ts(cb("bo1"), m16, col(2), None, OP.is_equal)
    ts(cb("u1"), row144, col(3), None, OP.is_equal)
    act(cb("u17"), cb("u1"), AF.Copy, scale=S17)
    ts(col(7), col(1), -4096.0, 61440.0 - 2.5 * S17, OP.mult, OP.add)
    act(cb("kb"), row128, scale=0.0, bias=col(7))
    ts(A("mxm", 0, 128), j128, 0.5, 2e9, OP.is_ge, OP.mult)
    ts(A("mxm", 0, 128), A("mxm", 0, 128), -1e9, None, OP.add)
    ts(col(12), col(5), 10000.0, col(0), OP.mult, OP.add)
    ts(col(13), col(5), -10000.0, col(0), OP.mult, OP.add)
    for g2 in range(2):
        for c2 in range(2):
            ts(cb("sl", 128 * (2 * g2 + c2), 128), row128, float(-16 * g2 if c2 == 0 else 16 * (1 - g2) - 10000), col(12 + c2),
               OP.add, OP.is_equal)
    act(cb("u32"), cb("u1"), AF.Copy, scale=32.0)
    ts(col(6), col(1), -8.0, None, OP.add)
    act(cb("pt"), row128, scale=0.0, bias=col(6))
    act(A("mnm", 0, 128), A("mxm", 0, 128), AF.Copy, scale=-1.0)
    iota(cb("io"), [[512, 256]], 0, 0)
    fill(col(16), BIG)
    ts(fu("dum"), fu("dum"), col(2), None, OP.subtract)
    ts(col(17), col(2), -10.0, None, OP.mult)
    ts(fu("v0w"), fu("v0w"), col(17), None, OP.add)
    ts(A("pc", 0, 8), A("dum", 0, 8), 16.0, float(8 - 16 * V), OP.mult, OP.add)
    act(A("u1f", 0, 144), cb("u1"), AF.Copy)
    ts(cb("on"), A("m32", 0, 128), col(4), None, OP.is_equal)
    ts(cb("lt"), row128, col(0), None, OP.is_ge)
    tt(cb("lt"), cb("lt"), cb("on"), OP.mult)
    act(cb("ones"), row128, scale=0.0, bias=1.0)
    act(cb("c13"), A("row", 0, 16), scale=0.0, bias=1344.0)
    if NSB < 16:
        act(cb("ih"), cb("i1"), AF.Copy, scale=0.5)
        act(cb("u64"), cb("u1"), AF.Copy, scale=64.0)
        act(cb("um32"), cb("u1"), AF.Copy, scale=-32.0)
        ts(cb("bv16"), j128, float(NSB), -16.0, OP.is_ge, OP.mult)
        tt(cb("bv16"), cb("bv16"), cb("bo1"), OP.mult)
        act(cb("bv32"), cb("bv16"), AF.Copy, scale=2.0)
    act(cb("m512"), row128, scale=0.0, bias=-512.0)
    act(cb("c75"), A("row", 0, 2), scale=0.0, bias=-7.5)
    ts(A("col", 40, 56), A("jr", 0, 16), col(1), None, OP.is_equal)
    for q in range(16):
        act(cb("rq", 128 * q, 128), cb("bo1"), AF.Copy, scale=col(40 + q))
    for c in range(NC):
        ts(A("wfl1", 16 * c, 16 * c + 8), cw("v0w", c), -1344.0, None, OP.add)
    act(A("wrp1", 0, L), A("v2", 0, L), scale=0.5, bias=-1344.5)
    cp(col(18), A("thi", 0, 1))
    ts(col(22), col(18), 32.0, col(6), OP.mult, OP.add)
    ts(col(23), col(22), -BIG, BIG, OP.mult, OP.add)
    act(cb("i1k"), cb("i1"), AF.Copy, scale=1024.0)
    act(cb("imh"), cb("i1"), AF.Copy, scale=-0.5)
    act(cb("i256"), cb("i1"), AF.Copy, scale=-256.0)
    act(cb("boh"), cb("bo1"), AF.Copy, scale=0.5)
    ts(cb("tri"), A("jr", 0, 256), col(1), 32768.0, OP.is_le, OP.mult)
    def pushes(t):
        for x, lo, hi, to in (("a", 1024, 2048, 0), ("b", 0, 1026, 1024)):
            remote(prv, A("tab%d" % t, lo, hi), A("rem%d" % t, to, to + hi - lo), nxt, "push%s%d" % (x, t), "pl%s%d" % (x, t),
                   256 * (hi - lo))

    pushes(0)

    def l2p(out, src):
        (nm, lo, hi), (sn, slo, shi) = out, src
        return [(cb("sl", 128 * (2 * g2 + c2), 128), A(sn, slo + g2, shi, 2), A(nm, lo + c2, hi, 2))
                for c2 in range(2) for g2 in range(2)]

    def l2wrap(out, src):
        prs = l2p(out, src)
        group(None, prs[:2])
        group(None, prs[2:])

    def l2direct(c, o, nm):
        a = NL * c
        lo = CBN["bo1"][0]
        bank = "ps%d" % (4 + c)
        for pa in range(4):
            for ib in range(4):
                out = ([(bank, 0, 1)], T[bank][32 * pa:32 * pa + 32, o + 2 * ib:o + 2 * ib + 2], 2)
                mm(out, A(nm, a + 32 * ib, a + 32 * ib + 32), A("cb", lo + 32 * pa, lo + 32 * pa + 32, 16), True, True)

    def clean_q(t, c, nm):
        x = ck(nm, c)
        prs = [(cb("i1"), x)]
        ts(ck("q0", c), x, 0.0, None, OP.is_equal)
        prs.append((cb("im"), ck("q0", c)))
        if t >= 2:
            ts(ck("qb", c), x, A("rb0", 0, 1), A("rb0", 1, 2), OP.is_equal, OP.mult)
            prs.append((cb("im"), ck("qb", c)))
        if t >= 1:
            ra = "ra%d" % (t - 1)
            ts(ck("qa", c), x, A(ra, 0, 1), A(ra, 1, 2), OP.is_equal, OP.mult)
            prs.append((cb("im"), ck("qa", c)))
        return prs

    def stage_v(t, c):
        a = NL * c
        if t == 0:
            cp(ck("kv", c), A("tab0", 10 * a, 10 * (a + NL), 10))
            ts(ck("bv", c), A("nb", 10 * a, 10 * (a + NL), 10), -1344.0, None, OP.add)
        else:
            vl = cw("wl%d" % (t - 1), c)
            act(ck("kv", c), ind(tabw(t), vl))
            ts(ck("bv", c), ind(A("nb", 0, V), vl), -1344.0, None, OP.add)
        group(KA(c, 0, 128), clean_q(t, c, "kv"))

    def stage_n(t, c):
        a = NL * c
        z = ck(zbuf(t), c)
        m = AC(c, 128, 256)
        mm(SM(c, 0, 128), cb("bo1" if t == 0 else "boh"), z, True, True)
        act(ck("zs", c), z, scale=1.0 if t == 0 else 0.5, bias=-0.5)
        ts(ck("yi", c), SM(c, 0, 128), col(36), float(t), OP.add, OP.add)
        ts(ck("yj", c), ck("yi", c), 15, None, OP.bitwise_and)
        ts(m, ck("yj", c), 0.0, None, OP.is_equal)
        tt(ck("nm", c), ck("bv", c), m, OP.mult)
        group(SM(c, 128, 136), [(U("u1", q), A("nm", a + q, a + NL, 16)) for q in range(16)])
        ts(cw("nl", c), SM(c, 128, 136), 1344.0, None, OP.add)
        cp(ck("cd", c), ind(A("nb", 0, V), cw("nl", c)))
        kc = "kc%d" % c
        for s in range(SUBK):
            act(A(kc, 2048 // SUBK * s, 2048 // SUBK * (s + 1)),
                ind(tabw(t), A("cd", a + 128 // SUBK * s, a + 128 // SUBK * (s + 1))))
        cp(ck("kn", c), ind(tabw(t), cw("nl", c)))
        l2direct(c, 160, "nm")
        tt(ck("e0", c), ck("kn", c), KA(c, 0, 128), OP.is_equal)
        l2direct(c, 168, "e0")
        ts(ck("cdh", c), ck("cd", c), -1344.0, None, OP.add)
        group(KA(c, 128, 256), clean_q(t, c, "kn"))
        if NSV:
            act(ck("kvp", c), KA(c, 0, 128), AF.Copy)
        if NSN:
            act(ck("knp", c), KA(c, 128, 256), AF.Copy)
        ts(cw("dk", c), SM(c, 168, 176), 2.5, 15 * S17, OP.is_ge, OP.mult)
        tt(cw("nk16", c), cw("dk", c), SM(c, 160, 168), OP.add)

    def stage_cmp(t, c):
        kc = "kc%d" % c
        a = NL * c
        for e, db, ns, neg, lo in (("e1%d" % c, "da%d" % c, NSV, "kvp", 0), ("e2%d" % c, "db%d" % c, NSN, "knp", 128)):
            out = SM(c, 384, 512) if lo == 0 else AC(c, 0, 128)
            for b in range(ns // 4):
                hi = 512 * (4 - b)
                bk = nb_[0] % 2
                nb_[0] += 1
                for j in range(4):
                    o = DB(bk, 128 * j, 128 * j + 128)
                    mm(o, cb("i1"), A(kc, 12 - 4 * b + j, 2048, 16), True, False)
                    mm(o, cb("im"), ck(neg, c), False, True)
                act(A(db, hi - 512, hi), DB(bk, 0, 512), AF.Copy)
                if b % EQB == EQB - 1:
                    w = 512 * EQB
                    ts(A(e, hi - 512, hi - 512 + w), A(db, hi - 512, hi - 512 + w), 0.0, None, OP.is_equal)
            mm(out, cb("i1"), ck("cdh", c), True, False)
            mm(out, cb("i1"), cb("kb"), False, False)
            for k in range(16):
                ek = A(e, 128 * k, 128 * k + 128)
                if k < 16 - ns:
                    tt(ek, A(kc, k, 2048, 16), KA(c, lo, lo + 128), OP.is_equal)
                mm(out, U("u17", k), ek, False, k == 15)
            if lo == 0:
                cp(ck("av", c), out)
        act(ck("kvr", c), KA(c, 0, 128), AF.Relu)
        tt(ck("val", c), ck("av", c), AC(c, 0, 128), OP.min)
        tr(ck("vt", c), ck("val", c))
        scan(ck("sc", c), A("mxm", 0, 128), ck("vt", c), OP.min, OP.max)
        tt(cw("tot", c), A("sc", a + 15, a + NL, 16), cw("nk16", c), OP.max)
        big = 1.5 * 2 ** 35
        ts(cw("th", c), cw("tot", c), big, -big, OP.add, OP.add)
        tt(cw("w16", c), cw("tot", c), cw("th", c), OP.subtract)
        ts(cw("fl", c), cw("tot", c), 350000.0 - 2.5 * S17, None, OP.is_lt)
        sm = "ps%d" % (4 + c)
        l2wrap((sm, 136, 144), ("w16", 8 * c, 8 * c + 8))
        l2wrap((sm, 144, 152), ("fl", 8 * c, 8 * c + 8))
        ts(cw("wl%d" % t, c), SM(c, 136, 144), 1344.0, None, OP.add)
        cp(A("wfl%d" % (t & 1), 16 * c, 16 * c + 16), SM(c, 136, 152))

    def stage_w(t, c):
        a = NL * c
        cp(ck("kw", c), ind(tabw(t), cw("wl%d" % t, c)))
        prs = [(cb("i1"), ck("kw", c))]
        if t >= 1:
            ra = A("ra%d" % (t - 1), 3, 4)
            ts(ck("qa", c), ck("kw", c), ra, ra, OP.is_equal, OP.mult)
            prs.append((cb("im"), ck("qa", c)))
        if t >= 2:
            rb = A("rb0", 0, 1)
            ts(ck("qb", c), ck("kw", c), rb, rb, OP.is_equal, OP.mult)
            prs.append((cb("im"), ck("qb", c)))
        kw = SM(c, 0, 128)
        group(kw, prs)
        tt(ck("pi", c), ck("v2", c), kw, OP.mult)
        ts(ck("pj", c), ck("pi", c), col(8), float(4 * t), OP.add, OP.add)
        ts(ck("pk", c), ck("pj", c), 2, PL - 1, OP.arith_shift_right, OP.bitwise_and)
        cp(ck("pl", c), ck("pk", c))
        for s in range(SUBX):
            act(A("xc%d" % c, 2048 // SUBX * s, 2048 // SUBX * (s + 1)),
                ind(A("X", 0, PL), A("pl", a + 128 // SUBX * s, a + 128 // SUBX * (s + 1))))
        tt(ck("pz", c), ck(zbuf(t), c), kw, OP.mult)
        act(ck("kwc", c), kw, AF.Copy)
        act(ck("hb", c), ck("kwc", c), AF.Relu, scale=-BIG, bias=col(16))
        for q in range(16):
            mm(SM(c, 256 + q, 512, 16), cb("rq", 128 * q, 128), A("wfl%d" % (t & 1), 16 * c, 16 * c + 16), True, True)
        act(ck("flr", c), SM(c, 384, 512), scale=-512.0)
        if t < NR - 1:
            act(ck("v2", c), SM(c, 256, 384), scale=2.0, bias=2689.0)
            vr = ck("wrp%d" % (t & 1), c)
            act(vr, SM(c, 256, 384), AF.Copy)
            tt(ck("wm", c), vr, AC(c, 128, 256), OP.mult)

    def stage_full(t):
        ts(fu("dr"), fu("tot"), 2.2e6 - 2.5 * S17, 2048.0, OP.is_gt, OP.mult)
        group(F1(0, 16), [(cb("lt"), fu("fl"))]
              + [(cb("on"), A("fl", 0, 16 - 2 * d), F1(2 * d, 16)) for d in range(1, 8)]
              + [(cb("i1k"), fu("fl")), (cb("i1"), fu("dr"))])
        ts(fu("iah"), F1(0, 16), 1024.0 + CAP + 0.5, 16384.0, OP.is_gt, OP.mult)
        vprev = "wfl%d" % ((t + 1) & 1)

        def node(lo):
            return [(cb("i1"), cb("c13"))] + [(cb("i1"), A(vprev, 16 * c, 16 * c + 8), F1(lo + 8 * c, lo + 8 * c + 8))
                                              for c in range(NC)] + l2p(("ps1", 384 + lo, 400 + lo), ("iah", 0, 16))
        group(F1(64, 80), [(A("u1f", 15 - q, 143 - q), A("pz", q, L, 16)) for q in range(16)])
        zs = 1.0 if t == 0 else 2.0
        big = 1.5 * 2 ** 34 * zs
        ts(fu("hH"), F1(64, 80), big, -big, OP.add, OP.add)
        tt(fu("h2"), F1(64, 80), fu("hH"), OP.subtract)
        ts(fu("sl2"), fu("h2"), 1.0 / zs, 1024.0, OP.mult, OP.add)
        tab = "tab%d" % (t + 1)
        act(A("src", 0, L), ind(A("rem%d" % t, 0, H + 1), fu("sl2")))
        if t < NR - 1:
            ones = [(cb("ones"), A("fl", j, j + 1)) for j in range(16)]
            group(F1(16, 17), ones)
            group(F1(17, 18), ones + [(cb("i1"), cb("c75", 0, 1))])
            b27 = 1.5 * 2 ** 27
            ts(A("fs", 2, 3), F1(17, 18), b27, -b27, OP.add, OP.add)
            tt(A("fs", 3, 4), F1(16, 17), A("fs", 2, 3), OP.subtract)
        if t > 0:
            group(F1(48, 64), node(48))
            act(fu("vb"), F1(48, 64), bias=-1344.0)
            ts(fu("vah"), F1(48, 64), -1344.0, None, OP.add)
            vr = "wrp%d" % ((t - 1) & 1)
            group(KA(0, 0, 256), [(cb("i1"), cb("tri"))]
                  + [(cb("i1"), fu("vah"), KA(0, q, 256, 16)) for q in range(16)])
            o = 0
            prs = [(cb("bo1"), A("ed", 0, L))]
            for c1 in range(15):
                n = L - 16 * (c1 + 1)
                if c1 < E3S:
                    act(A("e3", o, o + n), A(vr, L - n, L), scale=-1.0, bias=A("vb", c1, c1 + 1))
                    oe = o + n
                else:
                    ts(A("e3", o, o + n), A(vr, L - n, L), A("vb", c1, c1 + 1), None, OP.is_equal)
                prs.append((cb("bo1"), A("e3", o, o + n), KA(1, 256 - n, 256)))
                o += n
            tt(A("ed", 0, L), A(vr, 0, L), KA(0, 0, 256), OP.is_equal)
            if E3S:
                ts(A("e3", 0, oe), A("e3", 0, oe), 0.0, None, OP.is_equal)
            group(KA(1, 0, 256), prs)
            act(A("cnb", 0, L), KA(1, 0, 256), AF.Copy)
            group(F1(80, 96), node(80) + [(U("u17", q), A("cnb", q, L, 16)) for q in range(16)])
        else:
            group(F1(80, 96), node(80))
        tt(fu("sy"), fu("dum"), F1(80, 96), OP.min)
        cp(fu("sl"), fu("sy"))
        for c in range(NC):
            o = SM(c, 256, 384)
            for x in ("kwc", "src"):
                mm(o, cb("i1"), ck(x, c), True, False)
                if x == "src" and t >= 1:
                    ts(ck("sa", c), ck("src", c), A("rc%d" % (t - 1), 0, 1), A("rc%d" % (t - 1), 0, 1), OP.is_equal, OP.mult)
                    mm(o, cb("im"), ck("sa", c), False, False)
                if x == "src" and t >= 2:
                    ts(ck("sb", c), ck("src", c), A("ra0", 0, 1), A("ra0", 0, 1), OP.is_equal, OP.mult)
                    mm(o, cb("im"), ck("sb", c), False, False)
                if x == "src":
                    mm(o, cb("i1"), cb("m512"), False, False)
                mm(o, cb("i1" if x == "kwc" else "im"), ck("flr", c), False, False)
                mm(o, cb("i256"), ck("kvr", c), False, True)
                tt(ck("f1" if x == "kwc" else "fi", c), ck("kvr" if x == "kwc" else "f1", c), o, OP.max)
        cp(ind(A(tab, 0, REM), fu("sl")), A("fi", 0, L))
        if t < NR - 1:
            group(KA(0, 256, 512), [(cb("i1"), A("bv", 0, L)), (cb("im"), A("nm", 0, L)), (cb("i1"), A("wm", 0, L))])
            act(A("bn", 0, L), KA(0, 256, 512), bias=1344.0)
            cp(ind(A("nb", 0, REM), fu("sl")), A("bn", 0, L))
            pushes(t + 1)
            dma("y", A("tab%d" % (t + 2), 0, V), A(tab, 0, V), 2 * 128 * V)

    def stage_d(t, c):
        a = NL * c
        z = ck(zbuf(t), c)
        out = AC(c, 256, 384)
        xc = "xc%d" % c
        mm(out, cb("i1"), cb("pt"), True, False)
        if NSB < 16:
            mm(KA(c, 256, 384), cb("i1" if t == 0 else "ih"), z, True, True)
            mm(out, cb("bv32" if t == 0 else "bv16"), z, False, False)
        for b in range(NSB // 4):
            bk = nb_[0] % 2
            nb_[0] += 1
            for j in range(4):
                o = DB(bk, 128 * j, 128 * j + 128)
                mm(o, cb("i1"), A(xc, 4 * b + j, 2048, 16), True, False)
                mm(o, cb("im" if t == 0 else "imh"), z, False, True)
            act(A("mx%d" % c, 512 * b, 512 * b + 512), DB(bk, 0, 512), AF.Abs)
        for p in range(15, -1, -1):
            mxp = A("mx%d" % c, 128 * p, 128 * p + 128)
            if p >= NSB:
                x = A(xc, p, 2048, 16)
                mm(out, U("um32", p), x, False, False)
                tt(mxp, x, KA(c, 256, 384), OP.max)
            mm(out, U("u32" if p < NSB else "u64", p), mxp, False, p == 0)
        tr(ck("dt", c), out)
        scan(ck("ds", c), A("mnm", 0, 128), ck("dt", c), OP.max, OP.min)
        b28 = 1.5 * 2 ** 28
        last = A("ds", a + 15, a + NL, 16)
        ts(cw("pH", c), last, b28, -b28, OP.add, OP.add)
        tt(cw("p16", c), last, cw("pH", c), OP.subtract)
        group(SM(c, 152, 160), [(cb("i1"), A("pc", 0, 8))] + l2p(("ps%d" % (4 + c), 152, 160), ("p16", 8 * c, 8 * c + 8)))
        cp(cw("pw", c), SM(c, 152, 160))
        tt(ck("sz", c), ind(A(xc, 0, 2048), cw("pw", c)), ck("zs", c), OP.add)
        b24 = 1.5 * 2 ** 24
        if t < NR - 1:
            ts(ck("zb", c), ck("sz", c), b24, -b24, OP.add, OP.add)
        else:
            ts(ck("xm", c), ck("sz", c), b24, -b24, OP.add, OP.add)
            act(ck("yzf", c), ck("xm", c), AF.Copy, scale=0.5)
            dma("y", hbm("yz", a, a + NL), ck("yzf", c), 512 * NL)
        tc = col(23) if t == 0 else A("fs", 4 + t, 5 + t)
        act(ck("ug", c), out, AF.Relu, scale=BIG, bias=tc)
        group(SM(c, 0, 128), [(cb("i1"), ck("kwc", c)), (cb("i1"), cb("io", a, NL)), (cb("i1"), ck("hb", c)),
                              (cb("i1"), ck("ug", c))])
        red(A("rr", c, c + 1), SM(c, 0, 128), OP.min)

    BL = ((0, H), (H, V))

    def clean(tab, frm, nm, acc):
        bon[0] = -CLB
        for lo, hi in BL:
            ts(A(nm, lo, hi), A(frm, lo, hi), acc[0], acc[1], OP.is_equal, OP.mult)
        for lo, hi in BL:
            dma("g", A(tab, lo, hi), A(nm, lo, hi), 2 * 128 * (hi - lo) * 2, add=True)
        bon[0] = 0.0

    def stage_rv(t):
        ra = "ra%d" % t
        tt(A("rr", 2, 3), A("rr", 0, 1), A("rr", 1, 2), OP.min)
        ts(A("rr", 2, 3), A("rr", 2, 3), BIG, None, OP.min)
        b32 = 1.5 * 2 ** 32
        ts(A("rr", 3, 4), A("rr", 2, 3), b32, -b32, OP.add, OP.add)
        tt(A(ra, 0, 1), A("rr", 2, 3), A("rr", 3, 4), OP.subtract)
        if t < NR - 1:
            ts(A(ra, 1, 2), A(ra, 0, 1), 1.0, None, OP.add)
            rb = "rb%d" % t
            if t == 1:
                tt(A("rr", 4, 5), A(ra, 0, 1), A("rb0", 0, 1), OP.not_equal)
                tt(A(ra, 3, 4), A("rr", 4, 5), A(ra, 0, 1), OP.mult)
            else:
                cp(A(ra, 3, 4), A(ra, 0, 1))
            ts(A(ra, 2, 3), A(ra, 3, 4), -1.0, None, OP.mult)
            clean("tab%d" % (t + 2), "tab%d" % (t + 1), "cln", (A(ra, 3, 4), A(ra, 2, 3)))
            remote(nxt, A(ra, 0, 2), A(rb, 0, 2), prv, "rvs%d" % t, "rvl%d" % t, 1024)
            remote(prv, A(ra, 0, 2), A("rc%d" % t, 0, 2), nxt, "rws%d" % t, "rwl%d" % t, 1024)
            ts(A(rb, 2, 3), A(rb, 0, 1), -1.0, None, OP.mult)
        else:
            tt(A("rr", 4, 5), A(ra, 0, 1), A("rb1", 0, 1), OP.not_equal)
            tt(A("rr", 5, 6), A("rr", 4, 5), A(ra, 0, 1), OP.mult)
            ts(A("rr", 6, 7), A("rr", 5, 6), -1.0, None, OP.mult)
            for i in range(7):
                lo, hi = 384 * i, 384 * i + 384
                ts(A("cln", lo, hi), A("tab3", lo, hi), A("rr", 5, 6), A("rr", 6, 7), OP.is_equal, OP.mult)
                o = A("ps%d" % (6, 7, 2, 3)[i % 4], 0, 384)
                group(o, [(cb("i1"), A("tab3", lo, hi)), (cb("i1"), A("clb", lo, hi)), (cb("i1"), A("cln", lo, hi))])
                if i % 2:
                    cp(A("fin", lo, hi), o)
                else:
                    act(A("fin", lo, hi), o, AF.Copy)
            for q, lo, hi in (("y", 0, 768), ("s", 768, 1536), ("y", 1536, 2304), ("s", 2304, V)):
                dma(q, hbm("yk", lo, hi), A("fin", lo, hi), 256 * (hi - lo))

    stages = {"v": stage_v, "n": stage_n, "c": stage_cmp, "w": stage_w, "d": stage_d}

    def st(f, t, c):
        bon[0] = BT[f][c]
        stages[f](t, c)
        bon[0] = 0.0

    for t in range(NR):
        for c in range(NC):
            st("v", t, c)
            st("n", t, c)
        for c in range(NC):
            st("c", t, c)
            st("w", t, c)
        bon[0] = BT["f"][0]
        stage_full(t)
        bon[0] = 0.0
        if t == 1:
            clean("tab3", "tab2", "clb", (A("rb0", 0, 1), A("rb0", 2, 3)))
        if t == 2:
            bon[0] = -CLB
            for lo, hi in BL:
                ts(A("clb", lo, hi), A("tab3", lo, hi), A("rb1", 0, 1), A("rb1", 2, 3), OP.is_equal, OP.mult)
            bon[0] = 0.0
        for c in range(NC):
            st("d", t, c)
        if t < NR - 1:
            ts(A("fs", 5 + t, 6 + t), A("fs", 3, 4), -32.0 * BIG, col(23), OP.mult, OP.add)
        stage_rv(t)
    _emit(g, T, ops)


def _emit(g, T, ops):
    n = len(ops)
    succ = [[] for _ in range(n)]
    for i, o in enumerate(ops):
        if "after" in o:
            o["deps"][o["after"]] = False
        for j in o["deps"]:
            succ[j].append(i)
    prio = [0.0] * n
    for i in range(n - 1, -1, -1):
        o = ops[i]
        prio[i] = o["dur"] + o["lat"] + max([prio[s] for s in succ[i]], default=0.0)
    prio = [p + o["bon"] for p, o in zip(prio, ops)]
    left = [len(o["deps"]) for o in ops]
    fin = [0.0] * n
    qfree, ready, order = {}, {}, []
    est = [0.0] * n

    def push(i):
        o = ops[i]
        e = 0.0
        for j, hard in o["deps"].items():
            if "after" in o and j == o["after"]:
                e = max(e, fin[j])
            elif hard:
                e = max(e, fin[j] + WK)
        est[i] = e
        ready.setdefault(o["q"], []).append(i)
    for i in range(n):
        if left[i] == 0:
            push(i)
    while len(order) < n:
        best = None
        for q, rs in ready.items():
            if not rs:
                continue
            f = 0.0 if q == "ext" else qfree.get(q, 0.0)
            t0 = max(f, min(est[i] for i in rs))
            if best is None or t0 < best[0]:
                best = (t0, q)
        t0, q = best
        rs = ready[q]
        i = max([i for i in rs if est[i] <= t0 + 30.0], key=lambda k: (prio[k], -k))
        rs.remove(i)
        o = ops[i]
        st = max(t0, est[i])
        qfree[q] = st + o["dur"]
        fin[i] = st + o["dur"] + o["lat"]
        order.append(i)
        for s in succ[i]:
            left[s] -= 1
            if left[s] == 0:
                push(s)
    eng = {"v": g.vector, "s": g.scalar, "p": g.tensor, "g": g, "y": g.sync}
    known = {q: {} for q in eng}
    count, semof, clock = {}, {}, {}
    pos = {i: k for k, i in enumerate(order)}
    for i in order:
        o = ops[i]
        q = o["q"]
        if q == "ext":
            semof[i] = (o["sem"], o["val"])
            count[o["sem"]] = o["val"]
            clock[i] = {o["sem"]: o["val"]}
            continue
        kn = known[q]
        need = {}
        for j in sorted([j for j, hard in o["deps"].items() if hard], key=lambda j: -pos[j]):
            s, v = semof[j]
            if kn.get(s, 0) >= v:
                continue
            need[s] = max(need.get(s, 0), v)
            for s2, v2 in clock[j].items():
                if kn.get(s2, 0) < v2:
                    kn[s2] = v2
        for s, v in need.items():
            eng[q].wait_ge(T.sem[s], v)
        r = o["call"]()
        s = "q" + q if o["sem"] is None else o["sem"]
        count[s] = count.get(s, 0) + o["val"]
        if "remote" not in o:
            r.then_inc(T.sem[s], o["val"])
        semof[i] = (s, count[s])
        clock[i] = dict(kn)
        clock[i][s] = count[s]
    for s, v in count.items():
        if known["g"].get(s, 0) < v:
            g.wait_ge(T.sem[s], v)
